import numpy as np
import ml_dtypes


def mxq(x, axis, fmt="e4m3"):
    dtype, down = {"e4m3": (ml_dtypes.float8_e4m3fn, 7), "e5m2": (ml_dtypes.float8_e5m2, 14)}[fmt]
    v = np.moveaxis(np.asarray(x, np.float32).astype(ml_dtypes.bfloat16).astype(np.float64), axis, -1)
    blocks = v.reshape(v.shape[:-1] + (-1, 32))
    amax = np.abs(blocks).max(-1, keepdims=True)
    byte = np.maximum(np.where(amax > 0, np.frexp(amax)[1] - 1 + 127, 0) - down, 1)
    scale = np.exp2(byte - 127.0)
    codes = (blocks / scale).astype(np.float32).astype(dtype).astype(np.float64)
    return np.moveaxis((codes * scale).reshape(v.shape), -1, axis)


WIDE = False


def mx_kscale(k):
    if not WIDE:
        return np.ones(k)
    levels = np.array([10, -10, 5, -5, 0])
    if k % 512:
        return np.exp2(np.random.permutation(np.resize(levels, k // 32))).repeat(32)
    a = np.empty((k // 512, 16))
    for p in range(k // 512):
        a[p, :8] = np.random.permutation(np.resize(levels, 8))
        for g in range(8):
            far = levels[np.abs(levels - a[p, g]) >= 10]
            a[p, g + 8] = far[np.random.randint(len(far))]
    return np.exp2(a.ravel()).repeat(32)


def f64(x):
    return np.asarray(x).astype(np.float64)


def striped(idx):
    return np.tile(idx.reshape(-1, 16).T, (8, 1)).astype(np.uint16)


def unstriped(offs):
    return offs[:16].T.reshape(-1).astype(np.int64)


E2M1 = np.array([0.0, 0.5, 1.0, 1.5, 2.0, 3.0, 4.0, 6.0, -0.0, -0.5, -1.0, -1.5, -2.0, -3.0, -4.0, -6.0])


def pack_weight(w, fmt):
    k, n = w.shape
    w = f64(np.asarray(w, np.float32).astype(ml_dtypes.bfloat16)).reshape(k // 32, 32, n)
    amax = np.abs(w).max(1)
    if fmt == "e4m3":
        byte = np.frexp(amax)[1] - 1 + 127 - 7
    else:
        mant, ex = np.frexp(amax / 6.0)
        byte = np.where(mant > 0.5, ex, ex - 1) + 127
    byte = np.clip(np.where(amax > 0, byte, 1), 1, 254)
    scaled = (w * np.exp2(127.0 - byte)[:, None, :]).reshape(k, n).astype(np.float32)
    by_word = np.ascontiguousarray(scaled.reshape(k // 512, 128, 4, n).transpose(0, 1, 3, 2))
    if fmt == "e4m3":
        words = by_word.astype(ml_dtypes.float8_e4m3fn).view(np.uint8)
    else:
        c = by_word.astype(ml_dtypes.float4_e2m1fn).view(np.uint8) & 0xF
        words = (c[..., 0::2] | (c[..., 1::2] << 4)).reshape(k // 512, 128, 2 * n)
    return np.ascontiguousarray(words), np.ascontiguousarray(byte.astype(np.uint8).reshape(k // 512, 16, n))


def unpack_weight(words, scales, fmt):
    g, _, n = scales.shape
    words = np.ascontiguousarray(words).reshape(g, 128, n, -1)
    if fmt == "e4m3":
        vals = words.view(ml_dtypes.float8_e4m3fn).astype(np.float64)
    else:
        nib = np.empty((g, 128, n, 4), np.uint8)
        nib[..., 0::2] = words & 0xF
        nib[..., 1::2] = words >> 4
        vals = E2M1[nib]
    vals = vals * np.repeat(np.exp2(scales.astype(np.float64) - 127.0), 8, axis=1)[..., None]
    return vals.transpose(0, 1, 3, 2).reshape(g * 512, n)


K, T, E, C, N = 2048, 1280, 4, 256, 512
M = 256


def by_expert(wq, xq):
    return np.concatenate([wq[e].T @ xq[:, e * C:(e + 1) * C] for e in range(E)], axis=1)


def setup_inputs():
    n = np.random.standard_normal
    s = mx_kscale(K)[:, None]
    v = mx_kscale(N)
    x = pack_weight(n((K, T)) * s, "e4m3")
    return {
        "x_words": x[0],
        "x_scales": x[1],
        "w": (n((E, K, N)) / np.sqrt(K) / s[None] * v[None, None, :]).astype(np.float32),
        "wp": (n((N, M)) / np.sqrt(N) / v[:, None]).astype(np.float32),
        "gate": np.tile(np.random.uniform(0.2, 1.0, E * C), (N, 1)).astype(np.float32),
        "offs": striped(np.random.permutation(T)[:E * C]),
    }


def reference(x_words, x_scales, w, wp, gate, offs):
    idx = unstriped(offs)
    xq = unpack_weight(x_words, x_scales, "e4m3")[:, idx]
    y = by_expert(mxq(f64(w), 1, "e4m3"), xq)
    c = np.zeros((N, T))
    c[:, idx] = f64(gate) * y
    return mxq(f64(wp), 0, "e4m3").T @ mxq(c, 0, "e4m3")

@@ -1,0 +1,176 @@
+from contextlib import ExitStack
+
+import concourse.mybir as mybir
+from concourse.masks import make_identity
+
+K, T, E, C, N, M = 2048, 1280, 4, 256, 512, 256
+S = E * C
+P = 128
+PACK = 4
+PASSES = K // (P * PACK)
+
+FLOPS = 2 * K * N * S + 2 * N * M * T
+BYTES = 4 * E * K * N + K * T + K * T // 32 + 4 * N * M + 4 * S + 2 * P * S // 16 + 4 * M * T
+
+F32 = mybir.dt.float32
+BF16 = mybir.dt.bfloat16
+I32 = mybir.dt.int32
+U32 = mybir.dt.uint32
+U16 = mybir.dt.uint16
+U8 = mybir.dt.uint8
+FP8X4 = mybir.dt.float8_e4m3fn_x4
+COPY = mybir.ActivationFunctionType.Copy
+
+VECTOR_COLUMNS = 96
+
+
+def interleave(copy, grouped, raw, lo, hi):
+    copy(
+        out=grouped[:, lo:hi, :].rearrange("p (c i) j -> p c j i", i=4),
+        in_=raw[:, :, lo:hi].rearrange("p j (c i) -> p c j i", i=4),
+    )
+
+
+def quantize(nc, codes, scales, grouped):
+    nc.vector.quantize_mx(
+        out=codes[:].bitcast(FP8X4),
+        scales=scales[:],
+        in_=grouped[:].rearrange("p c j -> p (c j)"),
+    )
+
+
+def tile_moe_nxt_lin_none_kernel(
+    tc, x_words, x_scales, w, wp, gate, offs, out
+):
+    nc = tc.nc
+    with ExitStack() as ctx:
+        keep = ctx.enter_context(tc.tile_pool(name="keep", bufs=1))
+        ring = ctx.enter_context(tc.tile_pool(name="ring", bufs=4))
+        sums = ctx.enter_context(tc.psum_pool(name="sums", bufs=4))
+        turns = ctx.enter_context(tc.psum_pool(name="turns", bufs=2))
+        projs = ctx.enter_context(tc.psum_pool(name="projs", bufs=2))
+
+        offsets = keep.tile([P, S // 16], U16, name="offsets")
+        token_scales = keep.tile([P, T], U8, name="token_scales", align_bytes=64)
+        token_words = [keep.tile([P, T], I32, name=f"token_words{o}") for o in range(PASSES)]
+        w_raw = [
+            [keep.tile([P, PACK, N], F32, name=f"w_raw{e}_{o}") for o in range(PASSES)]
+            for e in range(E)
+        ]
+        wp_raw = keep.tile([P, PACK, M], F32, name="wp_raw")
+        gate_rows = keep.tile([P, P], F32, name="gate_rows")
+        windows = [keep.tile([P, T], F32, name=f"window{h}") for h in range(M // P)]
+        identity = keep.tile([P, P], F32, name="identity")
+
+        nc.vector.memset(token_scales[:].bitcast(I32), 0)
+        make_identity(nc, identity[:])
+        nc.scalar.dma_start(
+            out=gate_rows[:], in_=gate[0:16, :].rearrange("a (j c) -> (a j) c", c=P)
+        )
+        for q in range(4):
+            nc.scalar.dma_start(
+                out=token_scales[32 * q : 32 * q + 16, :].bitcast(I32),
+                in_=x_scales[:, 4 * q : 4 * q + 4, :].bitcast(I32),
+            )
+
+        def load_w(e, o):
+            rows = w[e, o * P * PACK : (o + 1) * P * PACK, :]
+            nc.sync.dma_start(out=w_raw[e][o][:], in_=rows.rearrange("(p j) n -> p j n", j=PACK))
+
+        def load_tokens(o):
+            words = x_words[o].rearrange("p t r -> p (t r)").bitcast(I32)
+            nc.sync.dma_start(out=token_words[o][:], in_=words)
+
+        load_w(0, 0)
+        nc.sync.dma_start(offsets[:], offs)
+        load_tokens(0)
+        for o in range(1, PASSES):
+            load_w(0, o)
+            load_tokens(o)
+        nc.sync.dma_start(out=wp_raw[:], in_=wp.rearrange("(p j) f -> p j f", j=PACK))
+        for e in range(1, E):
+            for o in range(PASSES):
+                load_w(e, o)
+
+        for window in windows:
+            nc.vector.memset(window[:], 0.0)
+
+        gate_turned = turns.tile([P, 2, 2, P], F32, name="turned")
+        nc.tensor.transpose(gate_turned[:, 0, 0, :], gate_rows[:], identity[:])
+        gate_cols = keep.tile([P, S // P], F32, name="gate_cols")
+        nc.scalar.activation(gate_cols[:], gate_turned[:, 0, 0, 0 : S // P], COPY)
+
+        wp_codes = keep.tile([P, M], U32, name="wp_codes", align_bytes=64)
+        wp_scales = keep.tile([P, M], U8, name="wp_scales", align_bytes=64)
+
+        for e in range(E):
+            slots = offsets[:, e * C // 16 : (e + 1) * C // 16]
+            slot_scales = keep.tile([P, C], U8, name=f"slot_scales{e}", align_bytes=64)
+            nc.vector.tensor_copy(out=slot_scales[:], in_=token_scales[:].indirect(slots))
+            banks = [sums.tile([P, N], F32, name="bank") for h in range(C // P)]
+            for o in range(PASSES):
+                slot_words = keep.tile([P, C], U32, name=f"slot_words{e}_{o}", align_bytes=64)
+                nc.vector.tensor_copy(
+                    out=slot_words[:], in_=token_words[o][:].bitcast(U32).indirect(slots)
+                )
+                grouped = ring.tile([P, N, PACK], BF16, name="grouped", align_bytes=64)
+                interleave(nc.vector.tensor_copy, grouped, w_raw[e][o], 0, VECTOR_COLUMNS)
+                interleave(nc.scalar.copy, grouped, w_raw[e][o], VECTOR_COLUMNS, N)
+                w_codes = ring.tile([P, N], U32, name="w_codes", align_bytes=64)
+                w_scales = ring.tile([P, N], U8, name="w_scales", align_bytes=64)
+                quantize(nc, w_codes, w_scales, grouped)
+                for h in range(C // P):
+                    nc.tensor.matmul_mx(
+                        out=banks[h][:],
+                        lhsT=slot_words[:, h * P : (h + 1) * P].bitcast(FP8X4),
+                        lhsT_scale=slot_scales[4 * o :, h * P : (h + 1) * P],
+                        rhs=w_codes[:].bitcast(FP8X4),
+                        rhs_scale=w_scales[:],
+                        start=(o == 0),
+                        stop=(o == PASSES - 1),
+                    )
+
+            if e == 0:
+                wp_grouped = keep.tile([P, M, PACK], BF16, name="wp_grouped", align_bytes=64)
+                interleave(nc.vector.tensor_copy, wp_grouped, wp_raw, 0, M)
+                quantize(nc, wp_codes, wp_scales, wp_grouped)
+
+            turned = turns.tile([P, 2, 2, P], F32, name="turned")
+            for h in range(C // P):
+                c_rows = ring.tile([P, N], BF16, name="c_rows")
+                col = e * (C // P) + h
+                nc.scalar.activation(
+                    c_rows[:].rearrange("s (u p r) -> s u p r", u=2, r=2),
+                    banks[h][:].rearrange("s (p u r) -> s u p r", u=2, r=2),
+                    COPY,
+                    scale=gate_cols[:, col : col + 1],
+                )
+                pairs = c_rows[:].bitcast(F32)
+                for u in range(2):
+                    nc.tensor.transpose(turned[:, h, u, :], pairs[:, u * P : (u + 1) * P], identity[:])
+            c_grouped = ring.tile([P, C, PACK], BF16, name="c_grouped", align_bytes=64)
+            nc.scalar.copy(
+                out=c_grouped[:].rearrange("p s j -> p (s j)").bitcast(F32).rearrange("p (h s u) -> p h s u", h=2, u=2),
+                in_=turned[:].rearrange("p h u s -> p h s u"),
+            )
+            c_codes = ring.tile([P, C], U32, name="c_codes", align_bytes=64)
+            c_scales = ring.tile([P, C], U8, name="c_scales", align_bytes=64)
+            quantize(nc, c_codes, c_scales, c_grouped)
+            proj = projs.tile([P, M // P, C], F32, name="proj")
+            for h in range(M // P):
+                nc.tensor.matmul_mx(
+                    out=proj[:, h, :],
+                    lhsT=wp_codes[:, h * P : (h + 1) * P].bitcast(FP8X4),
+                    lhsT_scale=wp_scales[:, h * P : (h + 1) * P],
+                    rhs=c_codes[:].bitcast(FP8X4),
+                    rhs_scale=c_scales[:],
+                    start=True,
+                    stop=True,
+                )
+            results = ring.tile([P, M // P, C], F32, name="results")
+            nc.scalar.copy(out=results[:], in_=proj[:])
+            for h in range(M // P):
+                nc.vector.tensor_copy(out=windows[h][:].indirect(slots), in_=results[:, h, :])
+
+        for h in range(M // P):
+            nc.sync.dma_start(out=out[h * P : (h + 1) * P, :], in_=windows[h][:])

@@ -8,9 +8,14 @@ S = E * C
 P = 128
 PACK = 4
 PASSES = K // (P * PACK)
+CHUNKS = E * PASSES
+HALVES = C // P
+ROW_GROUPS = M // P
+GATHER = 512
+LIST_ROWS = 16
 
 FLOPS = 2 * K * N * S + 2 * N * M * T
-BYTES = 4 * E * K * N + K * T + K * T // 32 + 4 * N * M + 4 * S + 2 * P * S // 16 + 4 * M * T
+BYTES = 4 * E * K * N + K * T + K * T // 32 + 4 * N * M + 4 * S + 2 * P * S // LIST_ROWS + 4 * M * T
 
 F32 = mybir.dt.float32
 BF16 = mybir.dt.bfloat16
@@ -21,22 +26,24 @@ U8 = mybir.dt.uint8
 FP8X4 = mybir.dt.float8_e4m3fn_x4
 COPY = mybir.ActivationFunctionType.Copy
 
-VECTOR_COLUMNS = 96
+VECTOR_COLUMNS = (0, 0, 0, 0, 288, 288, 256, 32, 256, 224, 256, 192, 224, 256, 0, 224)
+
+GATED_IN = (4, 8, 12)
+GROUPED_IN = (5, 9, 14)
+RESULTS_IN = ((6, 8), (11, 13), (14, 15))
+
+RING = 5
 
 
-def interleave(copy, grouped, raw, lo, hi):
+def interleave(copy, grouped, raw, first, last):
     copy(
-        out=grouped[:, lo:hi, :].rearrange("p (c i) j -> p c j i", i=4),
-        in_=raw[:, :, lo:hi].rearrange("p j (c i) -> p c j i", i=4),
+        out=grouped[:, first:last, :].rearrange("p (c i) j -> p c j i", i=4),
+        in_=raw[:, :, first:last].rearrange("p j (c i) -> p c j i", i=4),
     )
 
 
 def quantize(nc, codes, scales, grouped):
-    nc.vector.quantize_mx(
-        out=codes[:].bitcast(FP8X4),
-        scales=scales[:],
-        in_=grouped[:].rearrange("p c j -> p (c j)"),
-    )
+    nc.vector.quantize_mx(out=codes.bitcast(FP8X4), scales=scales, in_=grouped)
 
 
 def tile_moe_nxt_lin_none_kernel(
@@ -45,132 +52,200 @@ def tile_moe_nxt_lin_none_kernel(
     nc = tc.nc
     with ExitStack() as ctx:
         keep = ctx.enter_context(tc.tile_pool(name="keep", bufs=1))
-        ring = ctx.enter_context(tc.tile_pool(name="ring", bufs=4))
-        sums = ctx.enter_context(tc.psum_pool(name="sums", bufs=4))
+        ring = ctx.enter_context(tc.tile_pool(name="ring", bufs=RING))
+        sums = ctx.enter_context(tc.psum_pool(name="sums", bufs=2 * HALVES))
         turns = ctx.enter_context(tc.psum_pool(name="turns", bufs=2))
         projs = ctx.enter_context(tc.psum_pool(name="projs", bufs=2))
 
-        offsets = keep.tile([P, S // 16], U16, name="offsets")
+        offsets = keep.tile([P, S // LIST_ROWS], U16, name="offsets")
         token_scales = keep.tile([P, T], U8, name="token_scales", align_bytes=64)
         token_words = [keep.tile([P, T], I32, name=f"token_words{o}") for o in range(PASSES)]
-        w_raw = [
-            [keep.tile([P, PACK, N], F32, name=f"w_raw{e}_{o}") for o in range(PASSES)]
-            for e in range(E)
-        ]
+        w_raw = [keep.tile([P, PACK, N], F32, name=f"w_raw{i}", align_bytes=64) for i in range(CHUNKS)]
         wp_raw = keep.tile([P, PACK, M], F32, name="wp_raw")
         gate_rows = keep.tile([P, P], F32, name="gate_rows")
-        windows = [keep.tile([P, T], F32, name=f"window{h}") for h in range(M // P)]
+        windows = [keep.tile([P, T], F32, name=f"window{r}") for r in range(ROW_GROUPS)]
         identity = keep.tile([P, P], F32, name="identity")
 
         nc.vector.memset(token_scales[:].bitcast(I32), 0)
         make_identity(nc, identity[:])
-        nc.scalar.dma_start(
-            out=gate_rows[:], in_=gate[0:16, :].rearrange("a (j c) -> (a j) c", c=P)
-        )
-        for q in range(4):
-            nc.scalar.dma_start(
-                out=token_scales[32 * q : 32 * q + 16, :].bitcast(I32),
-                in_=x_scales[:, 4 * q : 4 * q + 4, :].bitcast(I32),
-            )
-
-        def load_w(e, o):
-            rows = w[e, o * P * PACK : (o + 1) * P * PACK, :]
-            nc.sync.dma_start(out=w_raw[e][o][:], in_=rows.rearrange("(p j) n -> p j n", j=PACK))
 
         def load_tokens(o):
             words = x_words[o].rearrange("p t r -> p (t r)").bitcast(I32)
             nc.sync.dma_start(out=token_words[o][:], in_=words)
 
-        load_w(0, 0)
+        def load_token_scales():
+            for quadrant in range(4):
+                nc.sync.dma_start(
+                    out=token_scales[32 * quadrant : 32 * quadrant + 16, :].bitcast(I32),
+                    in_=x_scales[:, 4 * quadrant : 4 * quadrant + 4, :].bitcast(I32),
+                )
+
+        def load_gate():
+            rows = gate[0 : P * P // S, :]
+            nc.sync.dma_start(out=gate_rows[:], in_=rows.rearrange("a (j c) -> (a j) c", c=P))
+
+        def load_chunk(i):
+            e, o = divmod(i, PASSES)
+            rows = w[e, o * P * PACK : (o + 1) * P * PACK, :]
+            nc.sync.dma_start(out=w_raw[i][:], in_=rows.rearrange("(p j) n -> p j n", j=PACK))
+
+        def load_wp():
+            nc.sync.dma_start(out=wp_raw[:], in_=wp.rearrange("(p j) f -> p j f", j=PACK))
+
         nc.sync.dma_start(offsets[:], offs)
         load_tokens(0)
-        for o in range(1, PASSES):
-            load_w(0, o)
-            load_tokens(o)
-        nc.sync.dma_start(out=wp_raw[:], in_=wp.rearrange("(p j) f -> p j f", j=PACK))
-        for e in range(1, E):
-            for o in range(PASSES):
-                load_w(e, o)
+        load_tokens(1)
+        load_token_scales()
+        load_gate()
+        load_chunk(0)
+        load_tokens(2)
+        load_chunk(1)
+        load_tokens(3)
+        load_chunk(2)
+        load_chunk(3)
+        load_wp()
+        for i in range(PASSES, CHUNKS):
+            load_chunk(i)
 
-        for window in windows:
-            nc.vector.memset(window[:], 0.0)
+        nc.vector.memset(windows[0][:], 0.0)
+        nc.gpsimd.memset(windows[1][:], 0.0)
 
-        gate_turned = turns.tile([P, 2, 2, P], F32, name="turned")
-        nc.tensor.transpose(gate_turned[:, 0, 0, :], gate_rows[:], identity[:])
-        gate_cols = keep.tile([P, S // P], F32, name="gate_cols")
-        nc.scalar.activation(gate_cols[:], gate_turned[:, 0, 0, 0 : S // P], COPY)
+        gate_bank = turns.tile([P, HALVES, 2, P], F32, name="turned")
+        nc.tensor.transpose(gate_bank[:, 0, 0, :], gate_rows[:], identity[:])
+        gate_columns = keep.tile([P, S // P], F32, name="gate_columns")
+        nc.scalar.activation(gate_columns[:], gate_bank[:, 0, 0, 0 : S // P], COPY)
 
+        wp_grouped = keep.tile([P, M, PACK], BF16, name="wp_grouped", align_bytes=64)
         wp_codes = keep.tile([P, M], U32, name="wp_codes", align_bytes=64)
         wp_scales = keep.tile([P, M], U8, name="wp_scales", align_bytes=64)
 
-        for e in range(E):
-            slots = offsets[:, e * C // 16 : (e + 1) * C // 16]
-            slot_scales = keep.tile([P, C], U8, name=f"slot_scales{e}", align_bytes=64)
-            nc.vector.tensor_copy(out=slot_scales[:], in_=token_scales[:].indirect(slots))
-            banks = [sums.tile([P, N], F32, name="bank") for h in range(C // P)]
-            for o in range(PASSES):
-                slot_words = keep.tile([P, C], U32, name=f"slot_words{e}_{o}", align_bytes=64)
-                nc.vector.tensor_copy(
-                    out=slot_words[:], in_=token_words[o][:].bitcast(U32).indirect(slots)
+        slot_scales, slot_words, banks, turned, projected = {}, {}, {}, {}, {}
+
+        def slot_offsets(first, count):
+            return offsets[:, first // LIST_ROWS : (first + count) // LIST_ROWS]
+
+        def gather_scales(g):
+            slot_scales[g] = keep.tile([P, GATHER], U8, name=f"slot_scales{g}", align_bytes=64)
+            window = token_scales[:].indirect(slot_offsets(g * GATHER, GATHER))
+            nc.vector.tensor_copy(out=slot_scales[g][:], in_=window)
+
+        def gather_words(g, o):
+            slot_words[g, o] = keep.tile([P, GATHER], U32, name=f"slot_words{g}_{o}", align_bytes=64)
+            window = token_words[o][:].bitcast(U32).indirect(slot_offsets(g * GATHER, GATHER))
+            nc.vector.tensor_copy(out=slot_words[g, o][:], in_=window)
+
+        def round_chunk(i):
+            grouped = ring.tile([P, N, PACK], BF16, name="grouped", align_bytes=64)
+            split = VECTOR_COLUMNS[i]
+            if split:
+                interleave(nc.vector.tensor_copy, grouped, w_raw[i], 0, split)
+            interleave(nc.scalar.copy, grouped, w_raw[i], split, N)
+            return grouped
+
+        def multiply_chunk(i, grouped):
+            e, o = divmod(i, PASSES)
+            if o == 0:
+                banks[e] = [sums.tile([P, N], F32, name="bank") for h in range(HALVES)]
+            w_codes = ring.tile([P, N], U32, name="w_codes", align_bytes=64)
+            w_scales = ring.tile([P, N], U8, name="w_scales", align_bytes=64)
+            quantize(nc, w_codes[:], w_scales[:], grouped[:].rearrange("p c j -> p (c j)"))
+            for h in range(HALVES):
+                g, first = divmod(e * C + h * P, GATHER)
+                nc.tensor.matmul_mx(
+                    out=banks[e][h][:],
+                    lhsT=slot_words[g, o][:, first : first + P].bitcast(FP8X4),
+                    lhsT_scale=slot_scales[g][4 * o :, first : first + P],
+                    rhs=w_codes[:].bitcast(FP8X4),
+                    rhs_scale=w_scales[:],
+                    start=(o == 0),
+                    stop=(o == PASSES - 1),
                 )
-                grouped = ring.tile([P, N, PACK], BF16, name="grouped", align_bytes=64)
-                interleave(nc.vector.tensor_copy, grouped, w_raw[e][o], 0, VECTOR_COLUMNS)
-                interleave(nc.scalar.copy, grouped, w_raw[e][o], VECTOR_COLUMNS, N)
-                w_codes = ring.tile([P, N], U32, name="w_codes", align_bytes=64)
-                w_scales = ring.tile([P, N], U8, name="w_scales", align_bytes=64)
-                quantize(nc, w_codes, w_scales, grouped)
-                for h in range(C // P):
-                    nc.tensor.matmul_mx(
-                        out=banks[h][:],
-                        lhsT=slot_words[:, h * P : (h + 1) * P].bitcast(FP8X4),
-                        lhsT_scale=slot_scales[4 * o :, h * P : (h + 1) * P],
-                        rhs=w_codes[:].bitcast(FP8X4),
-                        rhs_scale=w_scales[:],
-                        start=(o == 0),
-                        stop=(o == PASSES - 1),
-                    )
 
-            if e == 0:
-                wp_grouped = keep.tile([P, M, PACK], BF16, name="wp_grouped", align_bytes=64)
-                interleave(nc.vector.tensor_copy, wp_grouped, wp_raw, 0, M)
-                quantize(nc, wp_codes, wp_scales, wp_grouped)
+        def staging(i, first_row, rows, width, beside_gated=False):
+            if i == CHUNKS:
+                return keep.tile([P, rows, width], F32, name=f"last{first_row}_{width}", align_bytes=64)[:]
+            first = 0 if beside_gated or N - VECTOR_COLUMNS[i] < width else N - width
+            return w_raw[i][:, first_row : first_row + rows, first : first + width]
 
-            turned = turns.tile([P, 2, 2, P], F32, name="turned")
-            for h in range(C // P):
-                c_rows = ring.tile([P, N], BF16, name="c_rows")
-                col = e * (C // P) + h
+        def bank_parts(pool, shape, name, e):
+            if e == E - 1:
+                return [pool.tile(shape, F32, name=name)[:, 0:1] for part in range(2)]
+            return [pool.tile(shape, F32, name=name)[:]]
+
+        def gate_and_turn(e, i):
+            gated = staging(i, 0, 2 * HALVES, P)
+            turned[e] = bank_parts(turns, [P, HALVES, 2, P], "turned", e)
+            for h in range(HALVES):
+                pairs = gated[:, 2 * h : 2 * h + 2, :]
+                column = e * HALVES + h
                 nc.scalar.activation(
-                    c_rows[:].rearrange("s (u p r) -> s u p r", u=2, r=2),
-                    banks[h][:].rearrange("s (p u r) -> s u p r", u=2, r=2),
+                    pairs.bitcast(BF16).rearrange("s u (p r) -> s u p r", r=2),
+                    banks[e][h][:].rearrange("s (p u r) -> s u p r", u=2, r=2),
                     COPY,
-                    scale=gate_cols[:, col : col + 1],
+                    scale=gate_columns[:, column : column + 1],
                 )
-                pairs = c_rows[:].bitcast(F32)
+                part, index = divmod(h, HALVES // len(turned[e]))
                 for u in range(2):
-                    nc.tensor.transpose(turned[:, h, u, :], pairs[:, u * P : (u + 1) * P], identity[:])
-            c_grouped = ring.tile([P, C, PACK], BF16, name="c_grouped", align_bytes=64)
-            nc.scalar.copy(
-                out=c_grouped[:].rearrange("p s j -> p (s j)").bitcast(F32).rearrange("p (h s u) -> p h s u", h=2, u=2),
-                in_=turned[:].rearrange("p h u s -> p h s u"),
-            )
+                    nc.tensor.transpose(turned[e][part][:, index, u, :], pairs[:, u, :], identity[:])
+
+        def project(e, i):
+            c_grouped = staging(i, 0, HALVES, 2 * P)
             c_codes = ring.tile([P, C], U32, name="c_codes", align_bytes=64)
             c_scales = ring.tile([P, C], U8, name="c_scales", align_bytes=64)
-            quantize(nc, c_codes, c_scales, c_grouped)
-            proj = projs.tile([P, M // P, C], F32, name="proj")
-            for h in range(M // P):
+            per_part = HALVES // len(turned[e])
+            for part, bank in enumerate(turned[e]):
+                halves = range(part * per_part, (part + 1) * per_part)
+                nc.scalar.copy(
+                    out=c_grouped[:, halves.start : halves.stop, :].rearrange("p h (s u) -> p h s u", u=2),
+                    in_=bank.rearrange("p h u s -> p h s u"),
+                )
+                for h in halves:
+                    slots = slice(h * P, (h + 1) * P)
+                    quantize(nc, c_codes[:, slots], c_scales[:, slots], c_grouped[:, h, :].bitcast(BF16))
+            parts = bank_parts(projs, [P, ROW_GROUPS, C], "projected", e)
+            for r in range(ROW_GROUPS):
+                part, index = divmod(r, ROW_GROUPS // len(parts))
+                projected[e, r] = parts[part][:, index, :]
                 nc.tensor.matmul_mx(
-                    out=proj[:, h, :],
-                    lhsT=wp_codes[:, h * P : (h + 1) * P].bitcast(FP8X4),
-                    lhsT_scale=wp_scales[:, h * P : (h + 1) * P],
+                    out=projected[e, r],
+                    lhsT=wp_codes[:, r * P : (r + 1) * P].bitcast(FP8X4),
+                    lhsT_scale=wp_scales[:, r * P : (r + 1) * P],
                     rhs=c_codes[:].bitcast(FP8X4),
                     rhs_scale=c_scales[:],
                     start=True,
                     stop=True,
                 )
-            results = ring.tile([P, M // P, C], F32, name="results")
-            nc.scalar.copy(out=results[:], in_=proj[:])
-            for h in range(M // P):
-                nc.vector.tensor_copy(out=windows[h][:].indirect(slots), in_=results[:, h, :])
 
-        for h in range(M // P):
-            nc.sync.dma_start(out=out[h * P : (h + 1) * P, :], in_=windows[h][:])
+        def scatter(e, r, i):
+            results = staging(i, HALVES + r, 1, C, beside_gated=i in GATED_IN)[:, 0, :]
+            nc.scalar.copy(out=results, in_=projected[e, r])
+            nc.vector.tensor_copy(out=windows[r][:].indirect(slot_offsets(e * C, C)), in_=results)
+
+        gated_in = GATED_IN + (CHUNKS,)
+        grouped_in = GROUPED_IN + (CHUNKS,)
+        results_in = RESULTS_IN + ((CHUNKS, CHUNKS),)
+
+        for g in range(S // GATHER):
+            gather_scales(g)
+        for i in range(CHUNKS + 1):
+            if i < CHUNKS:
+                grouped = round_chunk(i)
+                if i < PASSES:
+                    gather_words(0, i)
+                multiply_chunk(i, grouped)
+            if i == 0:
+                interleave(nc.scalar.copy, wp_grouped, wp_raw, 0, M)
+                quantize(nc, wp_codes[:], wp_scales[:], wp_grouped[:].rearrange("p c j -> p (c j)"))
+            if i < PASSES:
+                gather_words(1, i)
+            for e in range(E):
+                if i == gated_in[e]:
+                    gate_and_turn(e, i)
+                if i == grouped_in[e]:
+                    project(e, i)
+                for r in range(ROW_GROUPS):
+                    if i == results_in[e][r]:
+                        scatter(e, r, i)
+
+        for r in range(ROW_GROUPS):
+            nc.sync.dma_start(out=out[r * P : (r + 1) * P, :], in_=windows[r][:])

@@ -26,13 +26,19 @@ U8 = mybir.dt.uint8
 FP8X4 = mybir.dt.float8_e4m3fn_x4
 COPY = mybir.ActivationFunctionType.Copy
 
-VECTOR_COLUMNS = (0, 0, 0, 0, 288, 288, 256, 32, 256, 224, 256, 192, 224, 256, 0, 224)
+VECTOR_COLUMNS = 256
+GPSIMD_COLUMNS = 224
 
-GATED_IN = (4, 8, 12)
-GROUPED_IN = (5, 9, 14)
-RESULTS_IN = ((6, 8), (11, 13), (14, 15))
-
+RUN_COLUMNS = 3 * N - 2 * GPSIMD_COLUMNS
 RING = 5
+
+
+def results_chunk(e, r):
+    return min(PASSES * (e + 2) - 1 + r, CHUNKS - 1)
+
+
+def beside_scatter(i):
+    return any(results_chunk(e, r) == i - 1 for e in range(E - 1) for r in range(ROW_GROUPS))
 
 
 def interleave(copy, grouped, raw, first, last):
@@ -53,7 +59,7 @@ def tile_moe_nxt_lin_none_kernel(
     with ExitStack() as ctx:
         keep = ctx.enter_context(tc.tile_pool(name="keep", bufs=1))
         ring = ctx.enter_context(tc.tile_pool(name="ring", bufs=RING))
-        sums = ctx.enter_context(tc.psum_pool(name="sums", bufs=2 * HALVES))
+        sums = ctx.enter_context(tc.psum_pool(name="sums", bufs=1))
         turns = ctx.enter_context(tc.psum_pool(name="turns", bufs=2))
         projs = ctx.enter_context(tc.psum_pool(name="projs", bufs=2))
 
@@ -119,7 +125,7 @@ def tile_moe_nxt_lin_none_kernel(
         wp_codes = keep.tile([P, M], U32, name="wp_codes", align_bytes=64)
         wp_scales = keep.tile([P, M], U8, name="wp_scales", align_bytes=64)
 
-        slot_scales, slot_words, banks, turned, projected = {}, {}, {}, {}, {}
+        slot_scales, slot_words, banks, turned, projected, run = {}, {}, {}, {}, {}, {}
 
         def slot_offsets(first, count):
             return offsets[:, first // LIST_ROWS : (first + count) // LIST_ROWS]
@@ -135,24 +141,43 @@ def tile_moe_nxt_lin_none_kernel(
             nc.vector.tensor_copy(out=slot_words[g, o][:], in_=window)
 
         def round_chunk(i):
-            grouped = ring.tile([P, N, PACK], BF16, name="grouped", align_bytes=64)
-            split = VECTOR_COLUMNS[i]
-            if split:
+            if beside_scatter(i):
+                run["first"] = run["first"] + N - GPSIMD_COLUMNS
+            else:
+                run["tile"] = ring.tile([P, RUN_COLUMNS, PACK], BF16, name="grouped", align_bytes=64, bufs=4)
+                run["first"] = 0
+            grouped = run["tile"][:, run["first"] : run["first"] + N, :]
+            split = 0
+            if beside_scatter(i):
+                split = GPSIMD_COLUMNS
+                nc.gpsimd.tensor_scalar(
+                    grouped[:, 0:split, :],
+                    w_raw[i][:, :, 0:split].rearrange("p j c -> p c j"),
+                    1.0,
+                    0.0,
+                    mybir.AluOpType.mult,
+                    mybir.AluOpType.add,
+                )
+            elif i >= PASSES:
+                split = VECTOR_COLUMNS
                 interleave(nc.vector.tensor_copy, grouped, w_raw[i], 0, split)
             interleave(nc.scalar.copy, grouped, w_raw[i], split, N)
             return grouped
 
-        def multiply_chunk(i, grouped):
+        def quantize_chunk(grouped):
+            w_codes = ring.tile([P, N], U32, name="w_codes", align_bytes=64, bufs=4)
+            w_scales = ring.tile([P, N], U8, name="w_scales", align_bytes=64)
+            quantize(nc, w_codes[:], w_scales[:], grouped.rearrange("p c j -> p (c j)"))
+            return w_codes, w_scales
+
+        def multiply_chunk(i, w_codes, w_scales):
             e, o = divmod(i, PASSES)
             if o == 0:
-                banks[e] = [sums.tile([P, N], F32, name="bank") for h in range(HALVES)]
-            w_codes = ring.tile([P, N], U32, name="w_codes", align_bytes=64)
-            w_scales = ring.tile([P, N], U8, name="w_scales", align_bytes=64)
-            quantize(nc, w_codes[:], w_scales[:], grouped[:].rearrange("p c j -> p (c j)"))
+                banks[e] = sums.tile([P, HALVES, N], F32, name="banks")
             for h in range(HALVES):
                 g, first = divmod(e * C + h * P, GATHER)
                 nc.tensor.matmul_mx(
-                    out=banks[e][h][:],
+                    out=banks[e][:, h, :],
                     lhsT=slot_words[g, o][:, first : first + P].bitcast(FP8X4),
                     lhsT_scale=slot_scales[g][4 * o :, first : first + P],
                     rhs=w_codes[:].bitcast(FP8X4),
@@ -161,11 +186,10 @@ def tile_moe_nxt_lin_none_kernel(
                     stop=(o == PASSES - 1),
                 )
 
-        def staging(i, first_row, rows, width, beside_gated=False):
-            if i == CHUNKS:
-                return keep.tile([P, rows, width], F32, name=f"last{first_row}_{width}", align_bytes=64)[:]
-            first = 0 if beside_gated or N - VECTOR_COLUMNS[i] < width else N - width
-            return w_raw[i][:, first_row : first_row + rows, first : first + width]
+        def staging(name, i, first_row, rows, width):
+            if i >= CHUNKS:
+                return keep.tile([P, rows, width], F32, name=f"last_{name}", align_bytes=64)[:]
+            return w_raw[i][:, first_row : first_row + rows, N - width : N]
 
         def bank_parts(pool, shape, name, e):
             if e == E - 1:
@@ -173,14 +197,14 @@ def tile_moe_nxt_lin_none_kernel(
             return [pool.tile(shape, F32, name=name)[:]]
 
         def gate_and_turn(e, i):
-            gated = staging(i, 0, 2 * HALVES, P)
+            gated = staging("gated", i, 0, HALVES, 2 * P)
             turned[e] = bank_parts(turns, [P, HALVES, 2, P], "turned", e)
             for h in range(HALVES):
-                pairs = gated[:, 2 * h : 2 * h + 2, :]
+                pairs = gated[:, h, :].rearrange("s (u p) -> s u p", u=2)
                 column = e * HALVES + h
                 nc.scalar.activation(
                     pairs.bitcast(BF16).rearrange("s u (p r) -> s u p r", r=2),
-                    banks[e][h][:].rearrange("s (p u r) -> s u p r", u=2, r=2),
+                    banks[e][:, h, :].rearrange("s (p u r) -> s u p r", u=2, r=2),
                     COPY,
                     scale=gate_columns[:, column : column + 1],
                 )
@@ -189,9 +213,9 @@ def tile_moe_nxt_lin_none_kernel(
                     nc.tensor.transpose(turned[e][part][:, index, u, :], pairs[:, u, :], identity[:])
 
         def project(e, i):
-            c_grouped = staging(i, 0, HALVES, 2 * P)
-            c_codes = ring.tile([P, C], U32, name="c_codes", align_bytes=64)
-            c_scales = ring.tile([P, C], U8, name="c_scales", align_bytes=64)
+            c_grouped = staging("grouped", i, 0, HALVES, 2 * P)
+            c_codes = ring.tile([P, C], U32, name="c_codes", align_bytes=64, bufs=2)
+            c_scales = ring.tile([P, C], U8, name="c_scales", align_bytes=64, bufs=2)
             per_part = HALVES // len(turned[e])
             for part, bank in enumerate(turned[e]):
                 halves = range(part * per_part, (part + 1) * per_part)
@@ -217,35 +241,35 @@ def tile_moe_nxt_lin_none_kernel(
                 )
 
         def scatter(e, r, i):
-            results = staging(i, HALVES + r, 1, C, beside_gated=i in GATED_IN)[:, 0, :]
+            results = staging(f"results{r}", i, HALVES + r, 1, C)[:, 0, :]
             nc.scalar.copy(out=results, in_=projected[e, r])
             nc.vector.tensor_copy(out=windows[r][:].indirect(slot_offsets(e * C, C)), in_=results)
 
-        gated_in = GATED_IN + (CHUNKS,)
-        grouped_in = GROUPED_IN + (CHUNKS,)
-        results_in = RESULTS_IN + ((CHUNKS, CHUNKS),)
-
         for g in range(S // GATHER):
             gather_scales(g)
-        for i in range(CHUNKS + 1):
-            if i < CHUNKS:
-                grouped = round_chunk(i)
-                if i < PASSES:
-                    gather_words(0, i)
-                multiply_chunk(i, grouped)
+        for i in range(CHUNKS):
+            grouped = round_chunk(i)
+            if i < PASSES:
+                gather_words(0, i)
+            w_codes, w_scales = quantize_chunk(grouped)
             if i == 0:
                 interleave(nc.scalar.copy, wp_grouped, wp_raw, 0, M)
                 quantize(nc, wp_codes[:], wp_scales[:], wp_grouped[:].rearrange("p c j -> p (c j)"))
             if i < PASSES:
                 gather_words(1, i)
-            for e in range(E):
-                if i == gated_in[e]:
-                    gate_and_turn(e, i)
-                if i == grouped_in[e]:
-                    project(e, i)
+            for e in range(E - 1):
                 for r in range(ROW_GROUPS):
-                    if i == results_in[e][r]:
+                    if i == results_chunk(e, r):
                         scatter(e, r, i)
+                if i == PASSES * (e + 1):
+                    gate_and_turn(e, i)
+                if i == PASSES * (e + 1) + 1:
+                    project(e, i)
+            multiply_chunk(i, w_codes, w_scales)
+        gate_and_turn(E - 1, CHUNKS)
+        project(E - 1, CHUNKS)
+        for r in range(ROW_GROUPS):
+            scatter(E - 1, r, CHUNKS)
 
         for r in range(ROW_GROUPS):
             nc.sync.dma_start(out=out[r * P : (r + 1) * P, :], in_=windows[r][:])

@@ -26,19 +26,25 @@ U8 = mybir.dt.uint8
 FP8X4 = mybir.dt.float8_e4m3fn_x4
 COPY = mybir.ActivationFunctionType.Copy
 
-VECTOR_COLUMNS = 256
-GPSIMD_COLUMNS = 224
+VECTOR_COLUMNS = 288
+GPSIMD_COLUMNS = 192
 
 RUN_COLUMNS = 3 * N - 2 * GPSIMD_COLUMNS
+EARLY_SLOTS = 128
 RING = 5
 
 
 def results_chunk(e, r):
-    return min(PASSES * (e + 2) - 1 + r, CHUNKS - 1)
+    return PASSES * (e + 1) + 2 + r if e < E - 2 else CHUNKS - 1
 
 
 def beside_scatter(i):
     return any(results_chunk(e, r) == i - 1 for e in range(E - 1) for r in range(ROW_GROUPS))
+
+
+def column_parts(e):
+    parts = 2 if e == E - 1 else 1
+    return [slice(a * N // parts, (a + 1) * N // parts) for a in range(parts)]
 
 
 def interleave(copy, grouped, raw, first, last):
@@ -73,6 +79,7 @@ def tile_moe_nxt_lin_none_kernel(
         identity = keep.tile([P, P], F32, name="identity")
 
         nc.vector.memset(token_scales[:].bitcast(I32), 0)
+        nc.vector.memset(gate_rows[:], 0.0)
         make_identity(nc, identity[:])
 
         def load_tokens(o):
@@ -87,8 +94,8 @@ def tile_moe_nxt_lin_none_kernel(
                 )
 
         def load_gate():
-            rows = gate[0 : P * P // S, :]
-            nc.sync.dma_start(out=gate_rows[:], in_=rows.rearrange("a (j c) -> (a j) c", c=P))
+            row = gate[0:1, :].rearrange("a (j c) -> (a j) c", c=P)
+            nc.sync.dma_start(out=gate_rows[0 : S // P, :], in_=row)
 
         def load_chunk(i):
             e, o = divmod(i, PASSES)
@@ -126,6 +133,9 @@ def tile_moe_nxt_lin_none_kernel(
         wp_scales = keep.tile([P, M], U8, name="wp_scales", align_bytes=64)
 
         slot_scales, slot_words, banks, turned, projected, run = {}, {}, {}, {}, {}, {}
+        gated_values = {}
+        zeros = keep.tile([P, EARLY_SLOTS], F32, name="zeros")
+        nc.gpsimd.memset(zeros[:], 0.0)
 
         def slot_offsets(first, count):
             return offsets[:, first // LIST_ROWS : (first + count) // LIST_ROWS]
@@ -144,7 +154,7 @@ def tile_moe_nxt_lin_none_kernel(
             if beside_scatter(i):
                 run["first"] = run["first"] + N - GPSIMD_COLUMNS
             else:
-                run["tile"] = ring.tile([P, RUN_COLUMNS, PACK], BF16, name="grouped", align_bytes=64, bufs=4)
+                run["tile"] = ring.tile([P, RUN_COLUMNS, PACK], BF16, name="grouped", align_bytes=64, bufs=3)
                 run["first"] = 0
             grouped = run["tile"][:, run["first"] : run["first"] + N, :]
             split = 0
@@ -158,33 +168,36 @@ def tile_moe_nxt_lin_none_kernel(
                     mybir.AluOpType.mult,
                     mybir.AluOpType.add,
                 )
-            elif i >= PASSES:
-                split = VECTOR_COLUMNS
+            elif i >= PASSES - 1:
+                split = VECTOR_COLUMNS if i < CHUNKS - 1 else N // 2
                 interleave(nc.vector.tensor_copy, grouped, w_raw[i], 0, split)
             interleave(nc.scalar.copy, grouped, w_raw[i], split, N)
             return grouped
 
-        def quantize_chunk(grouped):
+        def quantize_chunk(i, grouped):
             w_codes = ring.tile([P, N], U32, name="w_codes", align_bytes=64, bufs=4)
             w_scales = ring.tile([P, N], U8, name="w_scales", align_bytes=64)
-            quantize(nc, w_codes[:], w_scales[:], grouped.rearrange("p c j -> p (c j)"))
+            for columns in column_parts(i // PASSES if i == CHUNKS - 1 else 0):
+                values = grouped[:, columns, :].rearrange("p c j -> p (c j)")
+                quantize(nc, w_codes[:, columns], w_scales[:, columns], values)
             return w_codes, w_scales
 
         def multiply_chunk(i, w_codes, w_scales):
             e, o = divmod(i, PASSES)
             if o == 0:
-                banks[e] = sums.tile([P, HALVES, N], F32, name="banks")
-            for h in range(HALVES):
-                g, first = divmod(e * C + h * P, GATHER)
-                nc.tensor.matmul_mx(
-                    out=banks[e][:, h, :],
-                    lhsT=slot_words[g, o][:, first : first + P].bitcast(FP8X4),
-                    lhsT_scale=slot_scales[g][4 * o :, first : first + P],
-                    rhs=w_codes[:].bitcast(FP8X4),
-                    rhs_scale=w_scales[:],
-                    start=(o == 0),
-                    stop=(o == PASSES - 1),
-                )
+                banks[e] = sums.tile([P, len(column_parts(e)), HALVES, N], F32, name="banks")
+            for a, columns in enumerate(column_parts(e)):
+                for h in range(HALVES):
+                    g, first = divmod(e * C + h * P, GATHER)
+                    nc.tensor.matmul_mx(
+                        out=banks[e][:, a, h, columns],
+                        lhsT=slot_words[g, o][:, first : first + P].bitcast(FP8X4),
+                        lhsT_scale=slot_scales[g][4 * o :, first : first + P],
+                        rhs=w_codes[:, columns].bitcast(FP8X4),
+                        rhs_scale=w_scales[:, columns],
+                        start=(o == 0),
+                        stop=(o == PASSES - 1),
+                    )
 
         def staging(name, i, first_row, rows, width):
             if i >= CHUNKS:
@@ -198,19 +211,22 @@ def tile_moe_nxt_lin_none_kernel(
 
         def gate_and_turn(e, i):
             gated = staging("gated", i, 0, HALVES, 2 * P)
-            turned[e] = bank_parts(turns, [P, HALVES, 2, P], "turned", e)
-            for h in range(HALVES):
-                pairs = gated[:, h, :].rearrange("s (u p) -> s u p", u=2)
-                column = e * HALVES + h
-                nc.scalar.activation(
-                    pairs.bitcast(BF16).rearrange("s u (p r) -> s u p r", r=2),
-                    banks[e][:, h, :].rearrange("s (p u r) -> s u p r", u=2, r=2),
-                    COPY,
-                    scale=gate_columns[:, column : column + 1],
-                )
-                part, index = divmod(h, HALVES // len(turned[e]))
-                for u in range(2):
-                    nc.tensor.transpose(turned[e][part][:, index, u, :], pairs[:, u, :], identity[:])
+            gated_values[e] = gated
+            turned[e] = bank_parts(turns, [P, HALVES, 2, P], "turned", E - 1)
+            for a, columns in enumerate(column_parts(e)):
+                for h in range(HALVES):
+                    pairs = gated[:, h, :].rearrange("s (u p) -> s u p", u=2)
+                    words = pairs[:, :, columns.start // PACK : columns.stop // PACK]
+                    column = e * HALVES + h
+                    nc.scalar.activation(
+                        words.bitcast(BF16).rearrange("s u (p r) -> s u p r", r=2),
+                        banks[e][:, a, h, columns].rearrange("s (p u r) -> s u p r", u=2, r=2),
+                        COPY,
+                        scale=gate_columns[:, column : column + 1],
+                    )
+                    if columns.stop == N:
+                        for u in range(2):
+                            nc.tensor.transpose(turned[e][h][:, 0, u, :], pairs[:, u, :], identity[:])
 
         def project(e, i):
             c_grouped = staging("grouped", i, 0, HALVES, 2 * P)
@@ -226,6 +242,8 @@ def tile_moe_nxt_lin_none_kernel(
                 for h in halves:
                     slots = slice(h * P, (h + 1) * P)
                     quantize(nc, c_codes[:, slots], c_scales[:, slots], c_grouped[:, h, :].bitcast(BF16))
+            if e == E - 1:
+                scatter_late(gated_values[e][:, HALVES - 1, EARLY_SLOTS:C])
             parts = bank_parts(projs, [P, ROW_GROUPS, C], "projected", e)
             for r in range(ROW_GROUPS):
                 part, index = divmod(r, ROW_GROUPS // len(parts))
@@ -241,9 +259,20 @@ def tile_moe_nxt_lin_none_kernel(
                 )
 
         def scatter(e, r, i):
-            results = staging(f"results{r}", i, HALVES + r, 1, C)[:, 0, :]
-            nc.scalar.copy(out=results, in_=projected[e, r])
-            nc.vector.tensor_copy(out=windows[r][:].indirect(slot_offsets(e * C, C)), in_=results)
+            count = EARLY_SLOTS if (e, r) == (E - 2, ROW_GROUPS - 1) else C
+            results = staging(f"results{r}", i, HALVES + r, 1, C)[:, 0, 0:count]
+            nc.scalar.copy(out=results, in_=projected[e, r][:, 0:count])
+            window = windows[r][:].indirect(slot_offsets(e * C, count))
+            if count == C:
+                nc.vector.tensor_copy(out=window, in_=results)
+            else:
+                nc.vector.tensor_tensor(window, results, zeros[:], mybir.AluOpType.add)
+
+        def scatter_late(results):
+            e, r, count = E - 2, ROW_GROUPS - 1, C - EARLY_SLOTS
+            nc.scalar.copy(out=results, in_=projected[e, r][:, EARLY_SLOTS:C])
+            window = windows[r][:].indirect(slot_offsets(e * C + EARLY_SLOTS, count))
+            nc.vector.tensor_tensor(window, results, zeros[:], mybir.AluOpType.add)
 
         for g in range(S // GATHER):
             gather_scales(g)
@@ -251,7 +280,7 @@ def tile_moe_nxt_lin_none_kernel(
             grouped = round_chunk(i)
             if i < PASSES:
                 gather_words(0, i)
-            w_codes, w_scales = quantize_chunk(grouped)
+            w_codes, w_scales = quantize_chunk(i, grouped)
             if i == 0:
                 interleave(nc.scalar.copy, wp_grouped, wp_raw, 0, M)
                 quantize(nc, wp_codes[:], wp_scales[:], wp_grouped[:].rearrange("p c j -> p (c j)"))

@@ -31,6 +31,7 @@ GPSIMD_COLUMNS = 192
 
 RUN_COLUMNS = 3 * N - 2 * GPSIMD_COLUMNS
 EARLY_SLOTS = 128
+HEAD_COLUMNS = 192
 RING = 5
 
 
@@ -72,7 +73,9 @@ def tile_moe_nxt_lin_none_kernel(
         offsets = keep.tile([P, S // LIST_ROWS], U16, name="offsets")
         token_scales = keep.tile([P, T], U8, name="token_scales", align_bytes=64)
         token_words = [keep.tile([P, T], I32, name=f"token_words{o}") for o in range(PASSES)]
-        w_raw = [keep.tile([P, PACK, N], F32, name=f"w_raw{i}", align_bytes=64) for i in range(CHUNKS)]
+        w_raw = [keep.tile([P, PACK, N], F32, name=f"w_raw{i}", align_bytes=64) for i in range(CHUNKS - 1)]
+        head_raw = keep.tile([P, PACK, HEAD_COLUMNS], F32, name="head_raw", align_bytes=64)
+        tail_raw = keep.tile([P, PACK, N - HEAD_COLUMNS], F32, name="tail_raw", align_bytes=64)
         wp_raw = keep.tile([P, PACK, M], F32, name="wp_raw")
         gate_rows = keep.tile([P, P], F32, name="gate_rows")
         windows = [keep.tile([P, T], F32, name=f"window{r}") for r in range(ROW_GROUPS)]
@@ -100,7 +103,12 @@ def tile_moe_nxt_lin_none_kernel(
         def load_chunk(i):
             e, o = divmod(i, PASSES)
             rows = w[e, o * P * PACK : (o + 1) * P * PACK, :]
-            nc.sync.dma_start(out=w_raw[i][:], in_=rows.rearrange("(p j) n -> p j n", j=PACK))
+            rows = rows.rearrange("(p j) n -> p j n", j=PACK)
+            if i < CHUNKS - 1:
+                nc.sync.dma_start(out=w_raw[i][:], in_=rows)
+            else:
+                nc.sync.dma_start(out=head_raw[:], in_=rows[:, :, 0 : HEAD_COLUMNS])
+                nc.sync.dma_start(out=tail_raw[:], in_=rows[:, :, HEAD_COLUMNS:N])
 
         def load_wp():
             nc.sync.dma_start(out=wp_raw[:], in_=wp.rearrange("(p j) f -> p j f", j=PACK))
@@ -158,6 +166,12 @@ def tile_moe_nxt_lin_none_kernel(
                 run["first"] = 0
             grouped = run["tile"][:, run["first"] : run["first"] + N, :]
             split = 0
+            if i == CHUNKS - 1:
+                head, third = HEAD_COLUMNS, 104
+                interleave(nc.scalar.copy, grouped, head_raw, 0, head)
+                interleave(nc.vector.tensor_copy, grouped[:, head:N, :], tail_raw, third, N - head)
+                interleave(nc.scalar.copy, grouped[:, head:N, :], tail_raw, 0, third)
+                return grouped
             if beside_scatter(i):
                 split = GPSIMD_COLUMNS
                 nc.gpsimd.tensor_scalar(
@@ -169,7 +183,7 @@ def tile_moe_nxt_lin_none_kernel(
                     mybir.AluOpType.add,
                 )
             elif i >= PASSES - 1:
-                split = VECTOR_COLUMNS if i < CHUNKS - 1 else N // 2
+                split = VECTOR_COLUMNS
                 interleave(nc.vector.tensor_copy, grouped, w_raw[i], 0, split)
             interleave(nc.scalar.copy, grouped, w_raw[i], split, N)
             return grouped
@@ -200,6 +214,8 @@ def tile_moe_nxt_lin_none_kernel(
                     )
 
         def staging(name, i, first_row, rows, width):
+            if i == CHUNKS - 1:
+                return tail_raw[:, first_row : first_row + rows, 0:width]
             if i >= CHUNKS:
                 return keep.tile([P, rows, width], F32, name=f"last_{name}", align_bytes=64)[:]
             return w_raw[i][:, first_row : first_row + rows, N - width : N]

@@ -43,6 +43,10 @@ def beside_scatter(i):
     return any(results_chunk(e, r) == i - 1 for e in range(E - 1) for r in range(ROW_GROUPS))
 
 
+def sum_parts(e, h):
+    return column_parts(e) if h == 0 else [slice(0, N)]
+
+
 def column_parts(e):
     parts = 2 if e == E - 1 else 1
     return [slice(a * N // parts, (a + 1) * N // parts) for a in range(parts)]
@@ -141,7 +145,8 @@ def tile_moe_nxt_lin_none_kernel(
         wp_scales = keep.tile([P, M], U8, name="wp_scales", align_bytes=64)
 
         slot_scales, slot_words, banks, turned, projected, run = {}, {}, {}, {}, {}, {}
-        gated_values = {}
+        gated_values, last_codes = {}, {}
+        last_results = keep.tile([P, ROW_GROUPS, C], F32, name="last_results")
         zeros = keep.tile([P, EARLY_SLOTS], F32, name="zeros")
         nc.gpsimd.memset(zeros[:], 0.0)
 
@@ -199,12 +204,16 @@ def tile_moe_nxt_lin_none_kernel(
         def multiply_chunk(i, w_codes, w_scales):
             e, o = divmod(i, PASSES)
             if o == 0:
-                banks[e] = sums.tile([P, len(column_parts(e)), HALVES, N], F32, name="banks")
-            for a, columns in enumerate(column_parts(e)):
-                for h in range(HALVES):
+                both = sums.tile([P, HALVES, N], F32, name="banks")
+                banks[e] = {(0, h): both[:, h, :] for h in range(HALVES)}
+                if e == E - 1:
+                    banks[e][1, 0] = sums.tile([P, N], F32, name="second_part")[:]
+                    banks["warm"] = sums.tile([P, N], F32, name="warm")[:]
+            for h in range(HALVES):
+                for a, columns in enumerate(sum_parts(e, h)):
                     g, first = divmod(e * C + h * P, GATHER)
                     nc.tensor.matmul_mx(
-                        out=banks[e][:, a, h, columns],
+                        out=banks[e][a, h][:, columns],
                         lhsT=slot_words[g, o][:, first : first + P].bitcast(FP8X4),
                         lhsT_scale=slot_scales[g][4 * o :, first : first + P],
                         rhs=w_codes[:, columns].bitcast(FP8X4),
@@ -212,6 +221,21 @@ def tile_moe_nxt_lin_none_kernel(
                         start=(o == 0),
                         stop=(o == PASSES - 1),
                     )
+            last_codes["codes"], last_codes["scales"] = w_codes, w_scales
+            if i >= CHUNKS - 2:
+                for repeat in range(CHUNKS - i):
+                    warm_up(banks["warm"])
+
+        def warm_up(bank):
+            nc.tensor.matmul_mx(
+                out=bank,
+                lhsT=wp_codes[:, 0:P].bitcast(FP8X4),
+                lhsT_scale=wp_scales[:, 0:P],
+                rhs=last_codes["codes"][:].bitcast(FP8X4),
+                rhs_scale=last_codes["scales"][:],
+                start=True,
+                stop=True,
+            )
 
         def staging(name, i, first_row, rows, width):
             if i == CHUNKS - 1:
@@ -229,20 +253,22 @@ def tile_moe_nxt_lin_none_kernel(
             gated = staging("gated", i, 0, HALVES, 2 * P)
             gated_values[e] = gated
             turned[e] = bank_parts(turns, [P, HALVES, 2, P], "turned", E - 1)
-            for a, columns in enumerate(column_parts(e)):
-                for h in range(HALVES):
+            for h in range(HALVES):
+                for a, columns in enumerate(sum_parts(e, h)):
                     pairs = gated[:, h, :].rearrange("s (u p) -> s u p", u=2)
                     words = pairs[:, :, columns.start // PACK : columns.stop // PACK]
                     column = e * HALVES + h
                     nc.scalar.activation(
                         words.bitcast(BF16).rearrange("s u (p r) -> s u p r", r=2),
-                        banks[e][:, a, h, columns].rearrange("s (p u r) -> s u p r", u=2, r=2),
+                        banks[e][a, h][:, columns].rearrange("s (p u r) -> s u p r", u=2, r=2),
                         COPY,
                         scale=gate_columns[:, column : column + 1],
                     )
                     if columns.stop == N:
                         for u in range(2):
                             nc.tensor.transpose(turned[e][h][:, 0, u, :], pairs[:, u, :], identity[:])
+            if e == E - 1:
+                warm_up(banks[e][0, HALVES - 1])
 
         def project(e, i):
             c_grouped = staging("grouped", i, 0, HALVES, 2 * P)
@@ -260,6 +286,9 @@ def tile_moe_nxt_lin_none_kernel(
                     quantize(nc, c_codes[:, slots], c_scales[:, slots], c_grouped[:, h, :].bitcast(BF16))
             if e == E - 1:
                 scatter_late(gated_values[e][:, HALVES - 1, EARLY_SLOTS:C])
+                for h in range(HALVES):
+                    project_half(h, c_codes[:, h * P : (h + 1) * P], c_scales[:, h * P : (h + 1) * P])
+                return
             parts = bank_parts(projs, [P, ROW_GROUPS, C], "projected", e)
             for r in range(ROW_GROUPS):
                 part, index = divmod(r, ROW_GROUPS // len(parts))
@@ -273,6 +302,22 @@ def tile_moe_nxt_lin_none_kernel(
                     start=True,
                     stop=True,
                 )
+
+        def project_half(h, c_codes, c_scales):
+            bank = projs.tile([P, ROW_GROUPS, C], F32, name="projected")[:, :, 0:P]
+            for r in range(ROW_GROUPS):
+                nc.tensor.matmul_mx(
+                    out=bank[:, r, :],
+                    lhsT=wp_codes[:, r * P : (r + 1) * P].bitcast(FP8X4),
+                    lhsT_scale=wp_scales[:, r * P : (r + 1) * P],
+                    rhs=c_codes.bitcast(FP8X4),
+                    rhs_scale=c_scales,
+                    start=True,
+                    stop=True,
+                )
+            nc.scalar.copy(out=last_results[:, :, h * P : (h + 1) * P], in_=bank)
+            window = windows[0][:].indirect(slot_offsets((E - 1) * C + h * P, P))
+            nc.vector.tensor_tensor(window, last_results[:, 0, h * P : (h + 1) * P], zeros[:], mybir.AluOpType.add)
 
         def scatter(e, r, i):
             count = EARLY_SLOTS if (e, r) == (E - 2, ROW_GROUPS - 1) else C
@@ -313,8 +358,8 @@ def tile_moe_nxt_lin_none_kernel(
             multiply_chunk(i, w_codes, w_scales)
         gate_and_turn(E - 1, CHUNKS)
         project(E - 1, CHUNKS)
-        for r in range(ROW_GROUPS):
-            scatter(E - 1, r, CHUNKS)
+        window = windows[1][:].indirect(slot_offsets((E - 1) * C, C))
+        nc.vector.tensor_copy(out=window, in_=last_results[:, 1, :])
 
         for r in range(ROW_GROUPS):
             nc.sync.dma_start(out=out[r * P : (r + 1) * P, :], in_=windows[r][:])

@@ -26,12 +26,12 @@ U8 = mybir.dt.uint8
 FP8X4 = mybir.dt.float8_e4m3fn_x4
 COPY = mybir.ActivationFunctionType.Copy
 
-VECTOR_COLUMNS = 288
-GPSIMD_COLUMNS = 192
+VECTOR_COLUMNS = {0: 288, 1: 352, 2: 320, 3: 288}
+GPSIMD_COLUMNS = {0: 192, 3: 192}
 
-RUN_COLUMNS = 3 * N - 2 * GPSIMD_COLUMNS
+RUN_COLUMNS = 3 * N - sum(GPSIMD_COLUMNS.values())
 EARLY_SLOTS = 128
-HEAD_COLUMNS = 192
+HEAD_COLUMNS = 256
 RING = 5
 
 
@@ -77,9 +77,7 @@ def tile_moe_nxt_lin_none_kernel(
         offsets = keep.tile([P, S // LIST_ROWS], U16, name="offsets")
         token_scales = keep.tile([P, T], U8, name="token_scales", align_bytes=64)
         token_words = [keep.tile([P, T], I32, name=f"token_words{o}") for o in range(PASSES)]
-        w_raw = [keep.tile([P, PACK, N], F32, name=f"w_raw{i}", align_bytes=64) for i in range(CHUNKS - 1)]
-        head_raw = keep.tile([P, PACK, HEAD_COLUMNS], F32, name="head_raw", align_bytes=64)
-        tail_raw = keep.tile([P, PACK, N - HEAD_COLUMNS], F32, name="tail_raw", align_bytes=64)
+        w_raw = [keep.tile([P, PACK, N], F32, name=f"w_raw{i}", align_bytes=64) for i in range(CHUNKS)]
         wp_raw = keep.tile([P, PACK, M], F32, name="wp_raw")
         gate_rows = keep.tile([P, P], F32, name="gate_rows")
         windows = [keep.tile([P, T], F32, name=f"window{r}") for r in range(ROW_GROUPS)]
@@ -111,8 +109,8 @@ def tile_moe_nxt_lin_none_kernel(
             if i < CHUNKS - 1:
                 nc.sync.dma_start(out=w_raw[i][:], in_=rows)
             else:
-                nc.sync.dma_start(out=head_raw[:], in_=rows[:, :, 0 : HEAD_COLUMNS])
-                nc.sync.dma_start(out=tail_raw[:], in_=rows[:, :, HEAD_COLUMNS:N])
+                nc.sync.dma_start(out=w_raw[i][:, :, 0:HEAD_COLUMNS], in_=rows[:, :, 0 : HEAD_COLUMNS])
+                nc.sync.dma_start(out=w_raw[i][:, :, HEAD_COLUMNS:N], in_=rows[:, :, HEAD_COLUMNS:N])
 
         def load_wp():
             nc.sync.dma_start(out=wp_raw[:], in_=wp.rearrange("(p j) f -> p j f", j=PACK))
@@ -165,20 +163,19 @@ def tile_moe_nxt_lin_none_kernel(
 
         def round_chunk(i):
             if beside_scatter(i):
-                run["first"] = run["first"] + N - GPSIMD_COLUMNS
+                run["first"] = run["first"] + N - GPSIMD_COLUMNS[i % PASSES]
             else:
                 run["tile"] = ring.tile([P, RUN_COLUMNS, PACK], BF16, name="grouped", align_bytes=64, bufs=3)
                 run["first"] = 0
             grouped = run["tile"][:, run["first"] : run["first"] + N, :]
             split = 0
             if i == CHUNKS - 1:
-                head, third = HEAD_COLUMNS, 104
-                interleave(nc.scalar.copy, grouped, head_raw, 0, head)
-                interleave(nc.vector.tensor_copy, grouped[:, head:N, :], tail_raw, third, N - head)
-                interleave(nc.scalar.copy, grouped[:, head:N, :], tail_raw, 0, third)
+                interleave(nc.scalar.copy, grouped, w_raw[i], 0, 240)
+                interleave(nc.vector.tensor_copy, grouped, w_raw[i], 320, N)
+                interleave(nc.scalar.copy, grouped, w_raw[i], 240, 320)
                 return grouped
             if beside_scatter(i):
-                split = GPSIMD_COLUMNS
+                split = GPSIMD_COLUMNS[i % PASSES]
                 nc.gpsimd.tensor_scalar(
                     grouped[:, 0:split, :],
                     w_raw[i][:, :, 0:split].rearrange("p j c -> p c j"),
@@ -188,7 +185,7 @@ def tile_moe_nxt_lin_none_kernel(
                     mybir.AluOpType.add,
                 )
             elif i >= PASSES - 1:
-                split = VECTOR_COLUMNS
+                split = VECTOR_COLUMNS[i % PASSES]
                 interleave(nc.vector.tensor_copy, grouped, w_raw[i], 0, split)
             interleave(nc.scalar.copy, grouped, w_raw[i], split, N)
             return grouped
@@ -238,8 +235,6 @@ def tile_moe_nxt_lin_none_kernel(
             )
 
         def staging(name, i, first_row, rows, width):
-            if i == CHUNKS - 1:
-                return tail_raw[:, first_row : first_row + rows, 0:width]
             if i >= CHUNKS:
                 return keep.tile([P, rows, width], F32, name=f"last_{name}", align_bytes=64)[:]
             return w_raw[i][:, first_row : first_row + rows, N - width : N]
@@ -315,7 +310,11 @@ def tile_moe_nxt_lin_none_kernel(
                     start=True,
                     stop=True,
                 )
-            nc.scalar.copy(out=last_results[:, :, h * P : (h + 1) * P], in_=bank)
+            if h == 0:
+                for r in range(ROW_GROUPS):
+                    nc.scalar.copy(out=last_results[:, r, 0:P], in_=bank[:, r, :])
+            else:
+                nc.scalar.copy(out=last_results[:, :, h * P : (h + 1) * P], in_=bank)
             window = windows[0][:].indirect(slot_offsets((E - 1) * C + h * P, P))
             nc.vector.tensor_tensor(window, last_results[:, 0, h * P : (h + 1) * P], zeros[:], mybir.AluOpType.add)
 

@@ -26,17 +26,19 @@ U8 = mybir.dt.uint8
 FP8X4 = mybir.dt.float8_e4m3fn_x4
 COPY = mybir.ActivationFunctionType.Copy
 
-VECTOR_COLUMNS = {0: 288, 1: 352, 2: 320, 3: 288}
-GPSIMD_COLUMNS = {0: 192, 3: 192}
+VECTOR_COLUMNS = (288, 352, 320, 288)
+GPSIMD_COLUMNS = 192
+RUN_COLUMNS = 3 * N - 2 * GPSIMD_COLUMNS
 
-RUN_COLUMNS = 3 * N - sum(GPSIMD_COLUMNS.values())
-EARLY_SLOTS = 128
-HEAD_COLUMNS = 256
-RING = 5
+LAST = CHUNKS - 1
+LAST_OVERLAP = N // 2 - 16
+LAST_SPLIT = N // 2 + 64
+COLUMN_HALVES = (slice(0, N // 2), slice(N // 2, N))
+WHOLE = (slice(0, N),)
 
 
 def results_chunk(e, r):
-    return PASSES * (e + 1) + 2 + r if e < E - 2 else CHUNKS - 1
+    return PASSES * (e + 1) + 2 + r if e < E - 2 else LAST
 
 
 def beside_scatter(i):
@@ -44,12 +46,7 @@ def beside_scatter(i):
 
 
 def sum_parts(e, h):
-    return column_parts(e) if h == 0 else [slice(0, N)]
-
-
-def column_parts(e):
-    parts = 2 if e == E - 1 else 1
-    return [slice(a * N // parts, (a + 1) * N // parts) for a in range(parts)]
+    return COLUMN_HALVES if (e, h) == (E - 1, 0) else WHOLE
 
 
 def interleave(copy, grouped, raw, first, last):
@@ -69,7 +66,7 @@ def tile_moe_nxt_lin_none_kernel(
     nc = tc.nc
     with ExitStack() as ctx:
         keep = ctx.enter_context(tc.tile_pool(name="keep", bufs=1))
-        ring = ctx.enter_context(tc.tile_pool(name="ring", bufs=RING))
+        ring = ctx.enter_context(tc.tile_pool(name="ring", bufs=5))
         sums = ctx.enter_context(tc.psum_pool(name="sums", bufs=1))
         turns = ctx.enter_context(tc.psum_pool(name="turns", bufs=2))
         projs = ctx.enter_context(tc.psum_pool(name="projs", bufs=2))
@@ -106,11 +103,8 @@ def tile_moe_nxt_lin_none_kernel(
             e, o = divmod(i, PASSES)
             rows = w[e, o * P * PACK : (o + 1) * P * PACK, :]
             rows = rows.rearrange("(p j) n -> p j n", j=PACK)
-            if i < CHUNKS - 1:
-                nc.sync.dma_start(out=w_raw[i][:], in_=rows)
-            else:
-                nc.sync.dma_start(out=w_raw[i][:, :, 0:HEAD_COLUMNS], in_=rows[:, :, 0 : HEAD_COLUMNS])
-                nc.sync.dma_start(out=w_raw[i][:, :, HEAD_COLUMNS:N], in_=rows[:, :, HEAD_COLUMNS:N])
+            for columns in COLUMN_HALVES if i == LAST else WHOLE:
+                nc.sync.dma_start(out=w_raw[i][:, :, columns], in_=rows[:, :, columns])
 
         def load_wp():
             nc.sync.dma_start(out=wp_raw[:], in_=wp.rearrange("(p j) f -> p j f", j=PACK))
@@ -142,10 +136,10 @@ def tile_moe_nxt_lin_none_kernel(
         wp_codes = keep.tile([P, M], U32, name="wp_codes", align_bytes=64)
         wp_scales = keep.tile([P, M], U8, name="wp_scales", align_bytes=64)
 
-        slot_scales, slot_words, banks, turned, projected, run = {}, {}, {}, {}, {}, {}
-        gated_values, last_codes = {}, {}
+        slot_scales, slot_words, w_quantised = {}, {}, {}
+        banks, gated, turned, projected, run = {}, {}, {}, {}, {}
         last_results = keep.tile([P, ROW_GROUPS, C], F32, name="last_results")
-        zeros = keep.tile([P, EARLY_SLOTS], F32, name="zeros")
+        zeros = keep.tile([P, P], F32, name="zeros")
         nc.gpsimd.memset(zeros[:], 0.0)
 
         def slot_offsets(first, count):
@@ -163,19 +157,19 @@ def tile_moe_nxt_lin_none_kernel(
 
         def round_chunk(i):
             if beside_scatter(i):
-                run["first"] = run["first"] + N - GPSIMD_COLUMNS[i % PASSES]
+                run["first"] = run["first"] + N - GPSIMD_COLUMNS
             else:
                 run["tile"] = ring.tile([P, RUN_COLUMNS, PACK], BF16, name="grouped", align_bytes=64, bufs=3)
                 run["first"] = 0
             grouped = run["tile"][:, run["first"] : run["first"] + N, :]
-            split = 0
-            if i == CHUNKS - 1:
-                interleave(nc.scalar.copy, grouped, w_raw[i], 0, 240)
-                interleave(nc.vector.tensor_copy, grouped, w_raw[i], 320, N)
-                interleave(nc.scalar.copy, grouped, w_raw[i], 240, 320)
+            if i == LAST:
+                interleave(nc.scalar.copy, grouped, w_raw[i], 0, LAST_OVERLAP)
+                interleave(nc.vector.tensor_copy, grouped, w_raw[i], LAST_SPLIT, N)
+                interleave(nc.scalar.copy, grouped, w_raw[i], LAST_OVERLAP, LAST_SPLIT)
                 return grouped
+            split = 0
             if beside_scatter(i):
-                split = GPSIMD_COLUMNS[i % PASSES]
+                split = GPSIMD_COLUMNS
                 nc.gpsimd.tensor_scalar(
                     grouped[:, 0:split, :],
                     w_raw[i][:, :, 0:split].rearrange("p j c -> p c j"),
@@ -193,24 +187,25 @@ def tile_moe_nxt_lin_none_kernel(
         def quantize_chunk(i, grouped):
             w_codes = ring.tile([P, N], U32, name="w_codes", align_bytes=64, bufs=4)
             w_scales = ring.tile([P, N], U8, name="w_scales", align_bytes=64)
-            for columns in column_parts(i // PASSES if i == CHUNKS - 1 else 0):
+            for columns in COLUMN_HALVES if i == LAST else WHOLE:
                 values = grouped[:, columns, :].rearrange("p c j -> p (c j)")
                 quantize(nc, w_codes[:, columns], w_scales[:, columns], values)
-            return w_codes, w_scales
+            w_quantised[i] = (w_codes, w_scales)
 
-        def multiply_chunk(i, w_codes, w_scales):
+        def multiply_chunk(i):
             e, o = divmod(i, PASSES)
+            w_codes, w_scales = w_quantised[i]
             if o == 0:
                 both = sums.tile([P, HALVES, N], F32, name="banks")
-                banks[e] = {(0, h): both[:, h, :] for h in range(HALVES)}
+                banks[e] = {(h, 0): both[:, h, :] for h in range(HALVES)}
                 if e == E - 1:
-                    banks[e][1, 0] = sums.tile([P, N], F32, name="second_part")[:]
+                    banks[e][0, 1] = sums.tile([P, N], F32, name="extra_part")[:]
                     banks["warm"] = sums.tile([P, N], F32, name="warm")[:]
             for h in range(HALVES):
-                for a, columns in enumerate(sum_parts(e, h)):
-                    g, first = divmod(e * C + h * P, GATHER)
+                g, first = divmod(e * C + h * P, GATHER)
+                for part, columns in enumerate(sum_parts(e, h)):
                     nc.tensor.matmul_mx(
-                        out=banks[e][a, h][:, columns],
+                        out=banks[e][h, part][:, columns],
                         lhsT=slot_words[g, o][:, first : first + P].bitcast(FP8X4),
                         lhsT_scale=slot_scales[g][4 * o :, first : first + P],
                         rhs=w_codes[:, columns].bitcast(FP8X4),
@@ -218,120 +213,92 @@ def tile_moe_nxt_lin_none_kernel(
                         start=(o == 0),
                         stop=(o == PASSES - 1),
                     )
-            last_codes["codes"], last_codes["scales"] = w_codes, w_scales
-            if i >= CHUNKS - 2:
-                for repeat in range(CHUNKS - i):
-                    warm_up(banks["warm"])
 
-        def warm_up(bank):
+        def warm_up(bank, i):
+            w_codes, w_scales = w_quantised[i]
             nc.tensor.matmul_mx(
                 out=bank,
                 lhsT=wp_codes[:, 0:P].bitcast(FP8X4),
                 lhsT_scale=wp_scales[:, 0:P],
-                rhs=last_codes["codes"][:].bitcast(FP8X4),
-                rhs_scale=last_codes["scales"][:],
+                rhs=w_codes[:].bitcast(FP8X4),
+                rhs_scale=w_scales[:],
                 start=True,
                 stop=True,
             )
 
-        def staging(name, i, first_row, rows, width):
-            if i >= CHUNKS:
-                return keep.tile([P, rows, width], F32, name=f"last_{name}", align_bytes=64)[:]
-            return w_raw[i][:, first_row : first_row + rows, N - width : N]
-
-        def bank_parts(pool, shape, name, e):
-            if e == E - 1:
-                return [pool.tile(shape, F32, name=name)[:, 0:1] for part in range(2)]
-            return [pool.tile(shape, F32, name=name)[:]]
+        def staging(name, i, first_row, rows):
+            if i > LAST:
+                return keep.tile([P, rows, C], F32, name=f"last_{name}", align_bytes=64)[:]
+            return w_raw[i][:, first_row : first_row + rows, N - C : N]
 
         def gate_and_turn(e, i):
-            gated = staging("gated", i, 0, HALVES, 2 * P)
-            gated_values[e] = gated
-            turned[e] = bank_parts(turns, [P, HALVES, 2, P], "turned", E - 1)
+            gated[e] = staging("gated", i, 0, HALVES)
+            turned[e] = [turns.tile([P, HALVES, 2, P], F32, name="turned")[:, 0] for h in range(HALVES)]
             for h in range(HALVES):
-                for a, columns in enumerate(sum_parts(e, h)):
-                    pairs = gated[:, h, :].rearrange("s (u p) -> s u p", u=2)
+                pairs = gated[e][:, h, :].rearrange("s (u p) -> s u p", u=2)
+                column = e * HALVES + h
+                for part, columns in enumerate(sum_parts(e, h)):
                     words = pairs[:, :, columns.start // PACK : columns.stop // PACK]
-                    column = e * HALVES + h
                     nc.scalar.activation(
                         words.bitcast(BF16).rearrange("s u (p r) -> s u p r", r=2),
-                        banks[e][a, h][:, columns].rearrange("s (p u r) -> s u p r", u=2, r=2),
+                        banks[e][h, part][:, columns].rearrange("s (p u r) -> s u p r", u=2, r=2),
                         COPY,
                         scale=gate_columns[:, column : column + 1],
                     )
-                    if columns.stop == N:
-                        for u in range(2):
-                            nc.tensor.transpose(turned[e][h][:, 0, u, :], pairs[:, u, :], identity[:])
-            if e == E - 1:
-                warm_up(banks[e][0, HALVES - 1])
+                for u in range(2):
+                    nc.tensor.transpose(turned[e][h][:, u, :], pairs[:, u, :], identity[:])
 
-        def project(e, i):
-            c_grouped = staging("grouped", i, 0, HALVES, 2 * P)
+        def quantize_c(e, i):
+            c_grouped = staging("grouped", i, 0, HALVES)
             c_codes = ring.tile([P, C], U32, name="c_codes", align_bytes=64, bufs=2)
             c_scales = ring.tile([P, C], U8, name="c_scales", align_bytes=64, bufs=2)
-            per_part = HALVES // len(turned[e])
-            for part, bank in enumerate(turned[e]):
-                halves = range(part * per_part, (part + 1) * per_part)
+            for h in range(HALVES):
                 nc.scalar.copy(
-                    out=c_grouped[:, halves.start : halves.stop, :].rearrange("p h (s u) -> p h s u", u=2),
-                    in_=bank.rearrange("p h u s -> p h s u"),
+                    out=c_grouped[:, h, :].rearrange("p (s u) -> p s u", u=2),
+                    in_=turned[e][h].rearrange("p u s -> p s u"),
                 )
-                for h in halves:
-                    slots = slice(h * P, (h + 1) * P)
-                    quantize(nc, c_codes[:, slots], c_scales[:, slots], c_grouped[:, h, :].bitcast(BF16))
-            if e == E - 1:
-                scatter_late(gated_values[e][:, HALVES - 1, EARLY_SLOTS:C])
-                for h in range(HALVES):
-                    project_half(h, c_codes[:, h * P : (h + 1) * P], c_scales[:, h * P : (h + 1) * P])
-                return
-            parts = bank_parts(projs, [P, ROW_GROUPS, C], "projected", e)
-            for r in range(ROW_GROUPS):
-                part, index = divmod(r, ROW_GROUPS // len(parts))
-                projected[e, r] = parts[part][:, index, :]
-                nc.tensor.matmul_mx(
-                    out=projected[e, r],
-                    lhsT=wp_codes[:, r * P : (r + 1) * P].bitcast(FP8X4),
-                    lhsT_scale=wp_scales[:, r * P : (r + 1) * P],
-                    rhs=c_codes[:].bitcast(FP8X4),
-                    rhs_scale=c_scales[:],
-                    start=True,
-                    stop=True,
-                )
+                slots = slice(h * P, (h + 1) * P)
+                quantize(nc, c_codes[:, slots], c_scales[:, slots], c_grouped[:, h, :].bitcast(BF16))
+            return c_codes, c_scales
 
-        def project_half(h, c_codes, c_scales):
-            bank = projs.tile([P, ROW_GROUPS, C], F32, name="projected")[:, :, 0:P]
+        def multiply_wp(bank, r, c_codes, c_scales):
+            nc.tensor.matmul_mx(
+                out=bank,
+                lhsT=wp_codes[:, r * P : (r + 1) * P].bitcast(FP8X4),
+                lhsT_scale=wp_scales[:, r * P : (r + 1) * P],
+                rhs=c_codes.bitcast(FP8X4),
+                rhs_scale=c_scales,
+                start=True,
+                stop=True,
+            )
+
+        def project(e, c_codes, c_scales):
+            projected[e] = projs.tile([P, ROW_GROUPS, C], F32, name="projected")
             for r in range(ROW_GROUPS):
-                nc.tensor.matmul_mx(
-                    out=bank[:, r, :],
-                    lhsT=wp_codes[:, r * P : (r + 1) * P].bitcast(FP8X4),
-                    lhsT_scale=wp_scales[:, r * P : (r + 1) * P],
-                    rhs=c_codes.bitcast(FP8X4),
-                    rhs_scale=c_scales,
-                    start=True,
-                    stop=True,
-                )
-            if h == 0:
+                multiply_wp(projected[e][:, r, :], r, c_codes[:], c_scales[:])
+
+        def project_last(c_codes, c_scales):
+            for h in range(HALVES):
+                slots = slice(h * P, (h + 1) * P)
+                bank = projs.tile([P, ROW_GROUPS, C], F32, name="projected")[:, :, 0:P]
+                row_banks = [bank[:, r, :] for r in range(ROW_GROUPS)]
+                if h == HALVES - 1:
+                    row_banks[0] = sums.tile([P, N], F32, name="extra_part")[:, 0:P]
                 for r in range(ROW_GROUPS):
-                    nc.scalar.copy(out=last_results[:, r, 0:P], in_=bank[:, r, :])
-            else:
-                nc.scalar.copy(out=last_results[:, :, h * P : (h + 1) * P], in_=bank)
-            window = windows[0][:].indirect(slot_offsets((E - 1) * C + h * P, P))
-            nc.vector.tensor_tensor(window, last_results[:, 0, h * P : (h + 1) * P], zeros[:], mybir.AluOpType.add)
+                    multiply_wp(row_banks[r], r, c_codes[:, slots], c_scales[:, slots])
+                if h == HALVES - 1:
+                    for r in range(ROW_GROUPS):
+                        nc.scalar.copy(out=last_results[:, r, slots], in_=row_banks[r])
+                else:
+                    nc.scalar.copy(out=last_results[:, :, slots], in_=bank)
 
-        def scatter(e, r, i):
-            count = EARLY_SLOTS if (e, r) == (E - 2, ROW_GROUPS - 1) else C
-            results = staging(f"results{r}", i, HALVES + r, 1, C)[:, 0, 0:count]
-            nc.scalar.copy(out=results, in_=projected[e, r][:, 0:count])
-            window = windows[r][:].indirect(slot_offsets(e * C, count))
-            if count == C:
-                nc.vector.tensor_copy(out=window, in_=results)
-            else:
-                nc.vector.tensor_tensor(window, results, zeros[:], mybir.AluOpType.add)
+        def scatter(e, r, results):
+            nc.scalar.copy(out=results, in_=projected[e][:, r, :])
+            nc.vector.tensor_copy(out=windows[r][:].indirect(slot_offsets(e * C, C)), in_=results)
 
-        def scatter_late(results):
-            e, r, count = E - 2, ROW_GROUPS - 1, C - EARLY_SLOTS
-            nc.scalar.copy(out=results, in_=projected[e, r][:, EARLY_SLOTS:C])
-            window = windows[r][:].indirect(slot_offsets(e * C + EARLY_SLOTS, count))
+        def scatter_half(e, r, h, results):
+            nc.scalar.copy(out=results, in_=projected[e][:, r, h * P : (h + 1) * P])
+            window = windows[r][:].indirect(slot_offsets(e * C + h * P, P))
             nc.vector.tensor_tensor(window, results, zeros[:], mybir.AluOpType.add)
 
         for g in range(S // GATHER):
@@ -340,7 +307,7 @@ def tile_moe_nxt_lin_none_kernel(
             grouped = round_chunk(i)
             if i < PASSES:
                 gather_words(0, i)
-            w_codes, w_scales = quantize_chunk(i, grouped)
+            quantize_chunk(i, grouped)
             if i == 0:
                 interleave(nc.scalar.copy, wp_grouped, wp_raw, 0, M)
                 quantize(nc, wp_codes[:], wp_scales[:], wp_grouped[:].rearrange("p c j -> p (c j)"))
@@ -349,16 +316,28 @@ def tile_moe_nxt_lin_none_kernel(
             for e in range(E - 1):
                 for r in range(ROW_GROUPS):
                     if i == results_chunk(e, r):
-                        scatter(e, r, i)
+                        results = staging("results", i, HALVES + r, 1)[:, 0, :]
+                        if (e, r) == (E - 2, ROW_GROUPS - 1):
+                            scatter_half(e, r, 0, results[:, 0:P])
+                        else:
+                            scatter(e, r, results)
                 if i == PASSES * (e + 1):
                     gate_and_turn(e, i)
                 if i == PASSES * (e + 1) + 1:
-                    project(e, i)
-            multiply_chunk(i, w_codes, w_scales)
+                    project(e, *quantize_c(e, i))
+            multiply_chunk(i)
+            if i >= LAST - 1:
+                for repeat in range(CHUNKS - i):
+                    warm_up(banks["warm"], i)
+
         gate_and_turn(E - 1, CHUNKS)
-        project(E - 1, CHUNKS)
-        window = windows[1][:].indirect(slot_offsets((E - 1) * C, C))
-        nc.vector.tensor_copy(out=window, in_=last_results[:, 1, :])
+        warm_up(banks[E - 1][HALVES - 1, 0], LAST)
+        last_c = quantize_c(E - 1, CHUNKS)
+        scatter_half(E - 2, ROW_GROUPS - 1, 1, gated[E - 1][:, HALVES - 1, P:C])
+        project_last(*last_c)
+        for r in range(ROW_GROUPS):
+            window = windows[r][:].indirect(slot_offsets((E - 1) * C, C))
+            nc.vector.tensor_copy(out=window, in_=last_results[:, r, :])
 
         for r in range(ROW_GROUPS):
             nc.sync.dma_start(out=out[r * P : (r + 1) * P, :], in_=windows[r][:])

@@ -200,7 +200,6 @@ def tile_moe_nxt_lin_none_kernel(
                 banks[e] = {(h, 0): both[:, h, :] for h in range(HALVES)}
                 if e == E - 1:
                     banks[e][0, 1] = sums.tile([P, N], F32, name="extra_part")[:]
-                    banks["warm"] = sums.tile([P, N], F32, name="warm")[:]
             for h in range(HALVES):
                 g, first = divmod(e * C + h * P, GATHER)
                 for part, columns in enumerate(sum_parts(e, h)):
@@ -213,18 +212,6 @@ def tile_moe_nxt_lin_none_kernel(
                         start=(o == 0),
                         stop=(o == PASSES - 1),
                     )
-
-        def warm_up(bank, i):
-            w_codes, w_scales = w_quantised[i]
-            nc.tensor.matmul_mx(
-                out=bank,
-                lhsT=wp_codes[:, 0:P].bitcast(FP8X4),
-                lhsT_scale=wp_scales[:, 0:P],
-                rhs=w_codes[:].bitcast(FP8X4),
-                rhs_scale=w_scales[:],
-                start=True,
-                stop=True,
-            )
 
         def staging(name, i, first_row, rows):
             if i > LAST:
@@ -326,12 +313,8 @@ def tile_moe_nxt_lin_none_kernel(
                 if i == PASSES * (e + 1) + 1:
                     project(e, *quantize_c(e, i))
             multiply_chunk(i)
-            if i >= LAST - 1:
-                for repeat in range(CHUNKS - i):
-                    warm_up(banks["warm"], i)
 
         gate_and_turn(E - 1, CHUNKS)
-        warm_up(banks[E - 1][HALVES - 1, 0], LAST)
         last_c = quantize_c(E - 1, CHUNKS)
         scatter_half(E - 2, ROW_GROUPS - 1, 1, gated[E - 1][:, HALVES - 1, P:C])
         project_last(*last_c)

@@ -26,27 +26,19 @@ U8 = mybir.dt.uint8
 FP8X4 = mybir.dt.float8_e4m3fn_x4
 COPY = mybir.ActivationFunctionType.Copy
 
-VECTOR_COLUMNS = (288, 352, 320, 288)
-GPSIMD_COLUMNS = 192
-RUN_COLUMNS = 3 * N - 2 * GPSIMD_COLUMNS
-
 LAST = CHUNKS - 1
-LAST_OVERLAP = N // 2 - 16
-LAST_SPLIT = N // 2 + 64
 COLUMN_HALVES = (slice(0, N // 2), slice(N // 2, N))
 WHOLE = (slice(0, N),)
+RUN = 4
+RUN_SETS = N // (PACK * RUN)
+SCALAR_SETS = (32, 16, 0, 0)
 
 
-def results_chunk(e, r):
-    return PASSES * (e + 1) + 2 + r if e < E - 2 else LAST
-
-
-def beside_scatter(i):
-    return any(results_chunk(e, r) == i - 1 for e in range(E - 1) for r in range(ROW_GROUPS))
-
-
-def sum_parts(e, h):
-    return COLUMN_HALVES if (e, h) == (E - 1, 0) else WHOLE
+def round_w(copy, grouped, raw, tiles, sets):
+    copy(
+        out=grouped[:].rearrange("p t (a i) j -> p t a j i", i=RUN)[:, tiles, sets],
+        in_=raw[:].rearrange("p j (a t i) -> p t a j i", t=PACK, i=RUN)[:, tiles, sets],
+    )
 
 
 def interleave(copy, grouped, raw, first, last):
@@ -66,10 +58,8 @@ def tile_moe_nxt_lin_none_kernel(
     nc = tc.nc
     with ExitStack() as ctx:
         keep = ctx.enter_context(tc.tile_pool(name="keep", bufs=1))
-        ring = ctx.enter_context(tc.tile_pool(name="ring", bufs=5))
-        sums = ctx.enter_context(tc.psum_pool(name="sums", bufs=1))
-        turns = ctx.enter_context(tc.psum_pool(name="turns", bufs=2))
-        projs = ctx.enter_context(tc.psum_pool(name="projs", bufs=2))
+        ring = ctx.enter_context(tc.tile_pool(name="ring", bufs=3))
+        psum = ctx.enter_context(tc.psum_pool(name="psum", bufs=2))
 
         offsets = keep.tile([P, S // LIST_ROWS], U16, name="offsets")
         token_scales = keep.tile([P, T], U8, name="token_scales", align_bytes=64)
@@ -107,7 +97,9 @@ def tile_moe_nxt_lin_none_kernel(
                 nc.sync.dma_start(out=w_raw[i][:, :, columns], in_=rows[:, :, columns])
 
         def load_wp():
-            nc.sync.dma_start(out=wp_raw[:], in_=wp.rearrange("(p j) f -> p j f", j=PACK))
+            rows = wp.rearrange("(a t i) f -> t a i f", t=PACK, i=RUN)
+            for t in range(PACK):
+                nc.sync.dma_start(out=wp_raw[:, t, :], in_=rows[t])
 
         nc.sync.dma_start(offsets[:], offs)
         load_tokens(0)
@@ -124,23 +116,26 @@ def tile_moe_nxt_lin_none_kernel(
         for i in range(PASSES, CHUNKS):
             load_chunk(i)
 
-        nc.vector.memset(windows[0][:], 0.0)
-        nc.gpsimd.memset(windows[1][:], 0.0)
+        for r in range(ROW_GROUPS):
+            nc.gpsimd.memset(windows[r][:], 0.0)
 
-        gate_bank = turns.tile([P, HALVES, 2, P], F32, name="turned")
-        nc.tensor.transpose(gate_bank[:, 0, 0, :], gate_rows[:], identity[:])
+        gate_bank = psum.tile([P, PACK, P], F32, name="spread", bufs=4)
+        nc.tensor.transpose(gate_bank[:, 0, :], gate_rows[:], identity[:])
         gate_columns = keep.tile([P, S // P], F32, name="gate_columns")
-        nc.scalar.activation(gate_columns[:], gate_bank[:, 0, 0, 0 : S // P], COPY)
+        nc.scalar.copy(out=gate_columns[:], in_=gate_bank[:, 0, 0 : S // P])
+        gates = keep.tile([P, S // P, P], F32, name="gates")
+        for first in range(0, S // P, PACK):
+            spread = psum.tile([P, PACK, P], F32, name="spread", bufs=4)
+            for j in range(PACK):
+                column = gate_columns[:, first + j : first + j + 1].to_broadcast([P, P])
+                nc.tensor.transpose(spread[:, j, :], column, identity[:])
+            nc.scalar.copy(out=gates[:, first : first + PACK, :], in_=spread[:])
 
         wp_grouped = keep.tile([P, M, PACK], BF16, name="wp_grouped", align_bytes=64)
         wp_codes = keep.tile([P, M], U32, name="wp_codes", align_bytes=64)
         wp_scales = keep.tile([P, M], U8, name="wp_scales", align_bytes=64)
 
-        slot_scales, slot_words, w_quantised = {}, {}, {}
-        banks, gated, turned, projected, run = {}, {}, {}, {}, {}
-        last_results = keep.tile([P, ROW_GROUPS, C], F32, name="last_results")
-        zeros = keep.tile([P, P], F32, name="zeros")
-        nc.gpsimd.memset(zeros[:], 0.0)
+        slot_scales, slot_words, banks, projected = {}, {}, {}, {}
 
         def slot_offsets(first, count):
             return offsets[:, first // LIST_ROWS : (first + count) // LIST_ROWS]
@@ -156,171 +151,109 @@ def tile_moe_nxt_lin_none_kernel(
             nc.vector.tensor_copy(out=slot_words[g, o][:], in_=window)
 
         def round_chunk(i):
-            if beside_scatter(i):
-                run["first"] = run["first"] + N - GPSIMD_COLUMNS
-            else:
-                run["tile"] = ring.tile([P, RUN_COLUMNS, PACK], BF16, name="grouped", align_bytes=64, bufs=3)
-                run["first"] = 0
-            grouped = run["tile"][:, run["first"] : run["first"] + N, :]
+            grouped = ring.tile([P, PACK, P, PACK], BF16, name="grouped", align_bytes=64)
+            half = RUN_SETS // 2
             if i == LAST:
-                interleave(nc.scalar.copy, grouped, w_raw[i], 0, LAST_OVERLAP)
-                interleave(nc.vector.tensor_copy, grouped, w_raw[i], LAST_SPLIT, N)
-                interleave(nc.scalar.copy, grouped, w_raw[i], LAST_OVERLAP, LAST_SPLIT)
+                round_w(nc.scalar.copy, grouped, w_raw[i], slice(0, 4), slice(0, half))
+                round_w(nc.vector.tensor_copy, grouped, w_raw[i], slice(0, 2), slice(half, RUN_SETS))
+                round_w(nc.vector.tensor_copy, grouped, w_raw[i], slice(2, 3), slice(half, RUN_SETS))
+                round_w(nc.scalar.copy, grouped, w_raw[i], slice(3, 4), slice(half, RUN_SETS))
                 return grouped
-            split = 0
-            if beside_scatter(i):
-                split = GPSIMD_COLUMNS
-                nc.gpsimd.tensor_scalar(
-                    grouped[:, 0:split, :],
-                    w_raw[i][:, :, 0:split].rearrange("p j c -> p c j"),
-                    1.0,
-                    0.0,
-                    mybir.AluOpType.mult,
-                    mybir.AluOpType.add,
-                )
-            elif i >= PASSES - 1:
-                split = VECTOR_COLUMNS[i % PASSES]
-                interleave(nc.vector.tensor_copy, grouped, w_raw[i], 0, split)
-            interleave(nc.scalar.copy, grouped, w_raw[i], split, N)
+            split = 0 if i < PASSES else RUN_SETS - SCALAR_SETS[i % PASSES]
+            if split > 0:
+                for first in range(0, PACK, 2):
+                    round_w(nc.vector.tensor_copy, grouped, w_raw[i], slice(first, first + 2), slice(0, split))
+            if split < RUN_SETS:
+                round_w(nc.scalar.copy, grouped, w_raw[i], slice(0, PACK), slice(split, RUN_SETS))
             return grouped
 
         def quantize_chunk(i, grouped):
-            w_codes = ring.tile([P, N], U32, name="w_codes", align_bytes=64, bufs=4)
-            w_scales = ring.tile([P, N], U8, name="w_scales", align_bytes=64)
-            for columns in COLUMN_HALVES if i == LAST else WHOLE:
-                values = grouped[:, columns, :].rearrange("p c j -> p (c j)")
+            if i >= PASSES and i % PASSES == 0:
+                w_codes = keep.tile([P, N], U32, name="codes_after_c", tag="c_bytes", align_bytes=64)
+            else:
+                w_codes = ring.tile([P, N], U32, name="w_codes", align_bytes=64, bufs=4)
+            w_scales = ring.tile([P, N], U8, name="w_scales", align_bytes=64, bufs=4)
+            words = grouped[:].rearrange("p t m j -> p (t m) j")
+            for columns in COLUMN_HALVES if i >= PASSES else WHOLE:
+                values = words[:, columns, :].rearrange("p c j -> p (c j)")
                 quantize(nc, w_codes[:, columns], w_scales[:, columns], values)
-            w_quantised[i] = (w_codes, w_scales)
+            return w_codes, w_scales
 
-        def multiply_chunk(i):
+        def multiply_chunk(i, w_codes, w_scales):
             e, o = divmod(i, PASSES)
-            w_codes, w_scales = w_quantised[i]
-            if o == 0:
-                both = sums.tile([P, HALVES, N], F32, name="banks")
-                banks[e] = {(h, 0): both[:, h, :] for h in range(HALVES)}
-                if e == E - 1:
-                    banks[e][0, 1] = sums.tile([P, N], F32, name="extra_part")[:]
+            for pair in range(2):
+                for h in range(HALVES):
+                    if (o, pair) == (0, 0):
+                        banks[e, h] = psum.tile([P, PACK, P], F32, name=f"sums{h}")
+                    g, first = divmod(e * C + h * P, GATHER)
+                    for t in range(2 * pair, 2 * pair + 2):
+                        nc.tensor.matmul_mx(
+                            out=banks[e, h][:, t, :],
+                            lhsT=w_codes[:, t * P : (t + 1) * P].bitcast(FP8X4),
+                            lhsT_scale=w_scales[:, t * P : (t + 1) * P],
+                            rhs=slot_words[g, o][:, first : first + P].bitcast(FP8X4),
+                            rhs_scale=slot_scales[g][4 * o :, first : first + P],
+                            start=((o, t) == (0, 0)),
+                            stop=((o, t) == (PASSES - 1, PACK - 1)),
+                        )
+
+        def gate_and_project(e):
+            c_grouped = keep.tile([P, HALVES, P, PACK], BF16, name="c_grouped", tag="c_bytes", align_bytes=64)
             for h in range(HALVES):
-                g, first = divmod(e * C + h * P, GATHER)
-                for part, columns in enumerate(sum_parts(e, h)):
-                    nc.tensor.matmul_mx(
-                        out=banks[e][h, part][:, columns],
-                        lhsT=slot_words[g, o][:, first : first + P].bitcast(FP8X4),
-                        lhsT_scale=slot_scales[g][4 * o :, first : first + P],
-                        rhs=w_codes[:, columns].bitcast(FP8X4),
-                        rhs_scale=w_scales[:, columns],
-                        start=(o == 0),
-                        stop=(o == PASSES - 1),
-                    )
-
-        def staging(name, i, first_row, rows):
-            if i > LAST:
-                return keep.tile([P, rows, C], F32, name=f"last_{name}", align_bytes=64)[:]
-            return w_raw[i][:, first_row : first_row + rows, N - C : N]
-
-        def gate_and_turn(e, i):
-            gated[e] = staging("gated", i, 0, HALVES)
-            turned[e] = [turns.tile([P, HALVES, 2, P], F32, name="turned")[:, 0] for h in range(HALVES)]
-            for h in range(HALVES):
-                pairs = gated[e][:, h, :].rearrange("s (u p) -> s u p", u=2)
-                column = e * HALVES + h
-                for part, columns in enumerate(sum_parts(e, h)):
-                    words = pairs[:, :, columns.start // PACK : columns.stop // PACK]
-                    nc.scalar.activation(
-                        words.bitcast(BF16).rearrange("s u (p r) -> s u p r", r=2),
-                        banks[e][h, part][:, columns].rearrange("s (p u r) -> s u p r", u=2, r=2),
-                        COPY,
-                        scale=gate_columns[:, column : column + 1],
-                    )
-                for u in range(2):
-                    nc.tensor.transpose(turned[e][h][:, u, :], pairs[:, u, :], identity[:])
-
-        def quantize_c(e, i):
-            c_grouped = staging("grouped", i, 0, HALVES)
+                nc.vector.tensor_tensor(
+                    c_grouped[:, h],
+                    banks[e, h][:].rearrange("p t s -> p s t"),
+                    gates[:, e * HALVES + h, :].unsqueeze(2).to_broadcast([P, P, PACK]),
+                    mybir.AluOpType.mult,
+                )
             c_codes = ring.tile([P, C], U32, name="c_codes", align_bytes=64, bufs=2)
             c_scales = ring.tile([P, C], U8, name="c_scales", align_bytes=64, bufs=2)
-            for h in range(HALVES):
-                nc.scalar.copy(
-                    out=c_grouped[:, h, :].rearrange("p (s u) -> p s u", u=2),
-                    in_=turned[e][h].rearrange("p u s -> p s u"),
-                )
-                slots = slice(h * P, (h + 1) * P)
-                quantize(nc, c_codes[:, slots], c_scales[:, slots], c_grouped[:, h, :].bitcast(BF16))
-            return c_codes, c_scales
-
-        def multiply_wp(bank, r, c_codes, c_scales):
-            nc.tensor.matmul_mx(
-                out=bank,
-                lhsT=wp_codes[:, r * P : (r + 1) * P].bitcast(FP8X4),
-                lhsT_scale=wp_scales[:, r * P : (r + 1) * P],
-                rhs=c_codes.bitcast(FP8X4),
-                rhs_scale=c_scales,
-                start=True,
-                stop=True,
-            )
-
-        def project(e, c_codes, c_scales):
-            projected[e] = projs.tile([P, ROW_GROUPS, C], F32, name="projected")
+            quantize(nc, c_codes[:], c_scales[:], c_grouped[:].rearrange("p h s t -> p (h s t)"))
             for r in range(ROW_GROUPS):
-                multiply_wp(projected[e][:, r, :], r, c_codes[:], c_scales[:])
+                projected[e, r] = psum.tile([P, C], F32, name="spread", bufs=4)
+                nc.tensor.matmul_mx(
+                    out=projected[e, r][:],
+                    lhsT=wp_codes[:, r * P : (r + 1) * P].bitcast(FP8X4),
+                    lhsT_scale=wp_scales[:, r * P : (r + 1) * P],
+                    rhs=c_codes[:].bitcast(FP8X4),
+                    rhs_scale=c_scales[:],
+                    start=True,
+                    stop=True,
+                )
 
-        def project_last(c_codes, c_scales):
-            for h in range(HALVES):
-                slots = slice(h * P, (h + 1) * P)
-                bank = projs.tile([P, ROW_GROUPS, C], F32, name="projected")[:, :, 0:P]
-                row_banks = [bank[:, r, :] for r in range(ROW_GROUPS)]
-                if h == HALVES - 1:
-                    row_banks[0] = sums.tile([P, N], F32, name="extra_part")[:, 0:P]
-                for r in range(ROW_GROUPS):
-                    multiply_wp(row_banks[r], r, c_codes[:, slots], c_scales[:, slots])
-                if h == HALVES - 1:
-                    for r in range(ROW_GROUPS):
-                        nc.scalar.copy(out=last_results[:, r, slots], in_=row_banks[r])
-                else:
-                    nc.scalar.copy(out=last_results[:, :, slots], in_=bank)
-
-        def scatter(e, r, results):
-            nc.scalar.copy(out=results, in_=projected[e][:, r, :])
-            nc.vector.tensor_copy(out=windows[r][:].indirect(slot_offsets(e * C, C)), in_=results)
-
-        def scatter_half(e, r, h, results):
-            nc.scalar.copy(out=results, in_=projected[e][:, r, h * P : (h + 1) * P])
-            window = windows[r][:].indirect(slot_offsets(e * C + h * P, P))
-            nc.vector.tensor_tensor(window, results, zeros[:], mybir.AluOpType.add)
+        def put_back(e, r, results):
+            window = windows[r][:].indirect(slot_offsets(e * C, C))
+            if (e, r) == (E - 1, 0):
+                nc.vector.tensor_copy(out=results, in_=projected[e, r][:])
+                nc.vector.tensor_copy(out=window, in_=results)
+            else:
+                nc.scalar.copy(out=results, in_=projected[e, r][:])
+                nc.scalar.activation(window, results, COPY)
 
         for g in range(S // GATHER):
             gather_scales(g)
         for i in range(CHUNKS):
+            e, o = divmod(i, PASSES)
             grouped = round_chunk(i)
             if i < PASSES:
                 gather_words(0, i)
-            quantize_chunk(i, grouped)
-            if i == 0:
-                interleave(nc.scalar.copy, wp_grouped, wp_raw, 0, M)
-                quantize(nc, wp_codes[:], wp_scales[:], wp_grouped[:].rearrange("p c j -> p (c j)"))
+            quantised = quantize_chunk(i, grouped)
             if i < PASSES:
                 gather_words(1, i)
-            for e in range(E - 1):
+            if e > 0 and o == 1:
                 for r in range(ROW_GROUPS):
-                    if i == results_chunk(e, r):
-                        results = staging("results", i, HALVES + r, 1)[:, 0, :]
-                        if (e, r) == (E - 2, ROW_GROUPS - 1):
-                            scatter_half(e, r, 0, results[:, 0:P])
-                        else:
-                            scatter(e, r, results)
-                if i == PASSES * (e + 1):
-                    gate_and_turn(e, i)
-                if i == PASSES * (e + 1) + 1:
-                    project(e, *quantize_c(e, i))
-            multiply_chunk(i)
-
-        gate_and_turn(E - 1, CHUNKS)
-        last_c = quantize_c(E - 1, CHUNKS)
-        scatter_half(E - 2, ROW_GROUPS - 1, 1, gated[E - 1][:, HALVES - 1, P:C])
-        project_last(*last_c)
+                    if (e - 1, r) != (E - 2, 1):
+                        put_back(e - 1, r, w_raw[i][:, r, N - C : N])
+            if i == LAST:
+                put_back(E - 2, 1, w_raw[i][:, 0, N - C : N])
+            multiply_chunk(i, *quantised)
+            if i == PASSES - 1:
+                interleave(nc.scalar.copy, wp_grouped, wp_raw, 0, M)
+                quantize(nc, wp_codes[:], wp_scales[:], wp_grouped[:].rearrange("p c j -> p (c j)"))
+            if o == PASSES - 1:
+                gate_and_project(e)
         for r in range(ROW_GROUPS):
-            window = windows[r][:].indirect(slot_offsets((E - 1) * C, C))
-            nc.vector.tensor_copy(out=window, in_=last_results[:, r, :])
+            put_back(E - 1, r, keep.tile([P, C], F32, name=f"last_results{r}")[:])
 
         for r in range(ROW_GROUPS):
             nc.sync.dma_start(out=out[r * P : (r + 1) * P, :], in_=windows[r][:])

@@ -31,13 +31,13 @@ COLUMN_HALVES = (slice(0, N // 2), slice(N // 2, N))
 WHOLE = (slice(0, N),)
 RUN = 4
 RUN_SETS = N // (PACK * RUN)
-SCALAR_SETS = (32, 16, 0, 0)
+SCALAR_TILES = (4, 2, 0, 0)
 
 
 def round_w(copy, grouped, raw, tiles, sets):
     copy(
-        out=grouped[:].rearrange("p t (a i) j -> p t a j i", i=RUN)[:, tiles, sets],
-        in_=raw[:].rearrange("p j (a t i) -> p t a j i", t=PACK, i=RUN)[:, tiles, sets],
+        out=grouped[:].rearrange("p t (a i) j -> p a t j i", i=RUN)[:, sets, tiles],
+        in_=raw[:].rearrange("p j (a t i) -> p a t j i", t=PACK, i=RUN)[:, sets, tiles],
     )
 
 
@@ -152,19 +152,19 @@ def tile_moe_nxt_lin_none_kernel(
 
         def round_chunk(i):
             grouped = ring.tile([P, PACK, P, PACK], BF16, name="grouped", align_bytes=64)
-            half = RUN_SETS // 2
+            every, first, second = slice(0, RUN_SETS), slice(0, RUN_SETS // 2), slice(RUN_SETS // 2, RUN_SETS)
             if i == LAST:
-                round_w(nc.scalar.copy, grouped, w_raw[i], slice(0, 4), slice(0, half))
-                round_w(nc.vector.tensor_copy, grouped, w_raw[i], slice(0, 2), slice(half, RUN_SETS))
-                round_w(nc.vector.tensor_copy, grouped, w_raw[i], slice(2, 3), slice(half, RUN_SETS))
-                round_w(nc.scalar.copy, grouped, w_raw[i], slice(3, 4), slice(half, RUN_SETS))
+                round_w(nc.vector.tensor_copy, grouped, w_raw[i], slice(0, 2), first)
+                round_w(nc.scalar.copy, grouped, w_raw[i], slice(2, 4), first)
+                round_w(nc.vector.tensor_copy, grouped, w_raw[i], slice(0, 2), second)
+                round_w(nc.vector.tensor_copy, grouped, w_raw[i], slice(2, 3), second)
+                round_w(nc.scalar.copy, grouped, w_raw[i], slice(3, 4), second)
                 return grouped
-            split = 0 if i < PASSES else RUN_SETS - SCALAR_SETS[i % PASSES]
-            if split > 0:
-                for first in range(0, PACK, 2):
-                    round_w(nc.vector.tensor_copy, grouped, w_raw[i], slice(first, first + 2), slice(0, split))
-            if split < RUN_SETS:
-                round_w(nc.scalar.copy, grouped, w_raw[i], slice(0, PACK), slice(split, RUN_SETS))
+            split = 0 if i < PASSES else PACK - (2 if i == LAST - 1 else SCALAR_TILES[i % PASSES])
+            for t in range(0, split, 2):
+                round_w(nc.vector.tensor_copy, grouped, w_raw[i], slice(t, t + 2), every)
+            if split < PACK:
+                round_w(nc.scalar.copy, grouped, w_raw[i], slice(split, PACK), every)
             return grouped
 
         def quantize_chunk(i, grouped):
@@ -197,38 +197,50 @@ def tile_moe_nxt_lin_none_kernel(
                             stop=((o, t) == (PASSES - 1, PACK - 1)),
                         )
 
+        def project(bank, r, c_codes, c_scales):
+            nc.tensor.matmul_mx(
+                out=bank,
+                lhsT=wp_codes[:, r * P : (r + 1) * P].bitcast(FP8X4),
+                lhsT_scale=wp_scales[:, r * P : (r + 1) * P],
+                rhs=c_codes.bitcast(FP8X4),
+                rhs_scale=c_scales,
+                start=True,
+                stop=True,
+            )
+
         def gate_and_project(e):
             c_grouped = keep.tile([P, HALVES, P, PACK], BF16, name="c_grouped", tag="c_bytes", align_bytes=64)
             for h in range(HALVES):
+                factors = gates[:, e * HALVES + h, :].rearrange("p (c i) -> p c i", i=RUN)
                 nc.vector.tensor_tensor(
-                    c_grouped[:, h],
-                    banks[e, h][:].rearrange("p t s -> p s t"),
-                    gates[:, e * HALVES + h, :].unsqueeze(2).to_broadcast([P, P, PACK]),
+                    c_grouped[:, h].rearrange("p (c i) t -> p c t i", i=RUN),
+                    banks[e, h][:].rearrange("p t (c i) -> p c t i", i=RUN),
+                    factors.unsqueeze(2).to_broadcast([P, P // RUN, PACK, RUN]),
                     mybir.AluOpType.mult,
                 )
             c_codes = ring.tile([P, C], U32, name="c_codes", align_bytes=64, bufs=2)
             c_scales = ring.tile([P, C], U8, name="c_scales", align_bytes=64, bufs=2)
-            quantize(nc, c_codes[:], c_scales[:], c_grouped[:].rearrange("p h s t -> p (h s t)"))
-            for r in range(ROW_GROUPS):
-                projected[e, r] = psum.tile([P, C], F32, name="spread", bufs=4)
-                nc.tensor.matmul_mx(
-                    out=projected[e, r][:],
-                    lhsT=wp_codes[:, r * P : (r + 1) * P].bitcast(FP8X4),
-                    lhsT_scale=wp_scales[:, r * P : (r + 1) * P],
-                    rhs=c_codes[:].bitcast(FP8X4),
-                    rhs_scale=c_scales[:],
-                    start=True,
-                    stop=True,
-                )
+            if e < E - 1:
+                quantize(nc, c_codes[:], c_scales[:], c_grouped[:].rearrange("p h s t -> p (h s t)"))
+                for r in range(ROW_GROUPS):
+                    projected[e, r] = psum.tile([P, C], F32, name="spread", bufs=4)
+                    project(projected[e, r][:], r, c_codes[:], c_scales[:])
+                return
+            results = [keep.tile([P, C], F32, name=f"last_results{r}") for r in range(ROW_GROUPS)]
+            for h in range(HALVES):
+                slots = slice(h * P, (h + 1) * P)
+                quantize(nc, c_codes[:, slots], c_scales[:, slots], c_grouped[:, h].rearrange("p s t -> p (s t)"))
+                for r in range(ROW_GROUPS):
+                    bank = psum.tile([P, P], F32, name="spread", bufs=4)
+                    project(bank[:], r, c_codes[:, slots], c_scales[:, slots])
+                    copy = nc.vector.tensor_copy if r == 0 else nc.scalar.copy
+                    copy(out=results[r][:, slots], in_=bank[:])
+            nc.vector.tensor_copy(out=windows[0][:].indirect(slot_offsets(e * C, C)), in_=results[0][:])
+            nc.scalar.activation(windows[1][:].indirect(slot_offsets(e * C, C)), results[1][:], COPY)
 
         def put_back(e, r, results):
-            window = windows[r][:].indirect(slot_offsets(e * C, C))
-            if (e, r) == (E - 1, 0):
-                nc.vector.tensor_copy(out=results, in_=projected[e, r][:])
-                nc.vector.tensor_copy(out=window, in_=results)
-            else:
-                nc.scalar.copy(out=results, in_=projected[e, r][:])
-                nc.scalar.activation(window, results, COPY)
+            nc.scalar.copy(out=results, in_=projected[e, r][:])
+            nc.scalar.activation(windows[r][:].indirect(slot_offsets(e * C, C)), results, COPY)
 
         for g in range(S // GATHER):
             gather_scales(g)
@@ -240,20 +252,15 @@ def tile_moe_nxt_lin_none_kernel(
             quantised = quantize_chunk(i, grouped)
             if i < PASSES:
                 gather_words(1, i)
-            if e > 0 and o == 1:
+            if e > 0 and o == (1 if e < E - 1 else PASSES - 1):
                 for r in range(ROW_GROUPS):
-                    if (e - 1, r) != (E - 2, 1):
-                        put_back(e - 1, r, w_raw[i][:, r, N - C : N])
-            if i == LAST:
-                put_back(E - 2, 1, w_raw[i][:, 0, N - C : N])
+                    put_back(e - 1, r, w_raw[i][:, r, N - C : N])
             multiply_chunk(i, *quantised)
             if i == PASSES - 1:
                 interleave(nc.scalar.copy, wp_grouped, wp_raw, 0, M)
                 quantize(nc, wp_codes[:], wp_scales[:], wp_grouped[:].rearrange("p c j -> p (c j)"))
             if o == PASSES - 1:
                 gate_and_project(e)
-        for r in range(ROW_GROUPS):
-            put_back(E - 1, r, keep.tile([P, C], F32, name=f"last_results{r}")[:])
 
         for r in range(ROW_GROUPS):
             nc.sync.dma_start(out=out[r * P : (r + 1) * P, :], in_=windows[r][:])

@@ -31,7 +31,7 @@ COLUMN_HALVES = (slice(0, N // 2), slice(N // 2, N))
 WHOLE = (slice(0, N),)
 RUN = 4
 RUN_SETS = N // (PACK * RUN)
-SCALAR_TILES = (4, 2, 0, 0)
+SCALAR_TILES = (2, 2, 0, 0)
 
 
 def round_w(copy, grouped, raw, tiles, sets):
@@ -160,7 +160,7 @@ def tile_moe_nxt_lin_none_kernel(
                 round_w(nc.vector.tensor_copy, grouped, w_raw[i], slice(2, 3), second)
                 round_w(nc.scalar.copy, grouped, w_raw[i], slice(3, 4), second)
                 return grouped
-            split = 0 if i < PASSES else PACK - (2 if i == LAST - 1 else SCALAR_TILES[i % PASSES])
+            split = 0 if i < PASSES else PACK - SCALAR_TILES[i % PASSES]
             for t in range(0, split, 2):
                 round_w(nc.vector.tensor_copy, grouped, w_raw[i], slice(t, t + 2), every)
             if split < PACK:
@@ -252,9 +252,12 @@ def tile_moe_nxt_lin_none_kernel(
             quantised = quantize_chunk(i, grouped)
             if i < PASSES:
                 gather_words(1, i)
-            if e > 0 and o == (1 if e < E - 1 else PASSES - 1):
+            if e > 0 and o == 1:
                 for r in range(ROW_GROUPS):
-                    put_back(e - 1, r, w_raw[i][:, r, N - C : N])
+                    if (e - 1, r) != (E - 2, 1):
+                        put_back(e - 1, r, w_raw[i][:, r, N - C : N])
+            if i == LAST:
+                put_back(E - 2, 1, w_raw[i][:, 0, N - C : N])
             multiply_chunk(i, *quantised)
             if i == PASSES - 1:
                 interleave(nc.scalar.copy, wp_grouped, wp_raw, 0, M)

@@ -28,16 +28,13 @@ COPY = mybir.ActivationFunctionType.Copy
 
 LAST = CHUNKS - 1
 COLUMN_HALVES = (slice(0, N // 2), slice(N // 2, N))
-WHOLE = (slice(0, N),)
-RUN = 4
-RUN_SETS = N // (PACK * RUN)
-SCALAR_TILES = (2, 2, 0, 0)
+SCALAR_PAIRS = (2, 1, 0, 0)
 
 
-def round_w(copy, grouped, raw, tiles, sets):
+def round_w(copy, grouped, raw, pair):
     copy(
-        out=grouped[:].rearrange("p t (a i) j -> p a t j i", i=RUN)[:, sets, tiles],
-        in_=raw[:].rearrange("p j (a t i) -> p a t j i", t=PACK, i=RUN)[:, sets, tiles],
+        out=grouped.rearrange("p (u v) (a i) j -> p u a j i v", v=2, i=2)[:, pair],
+        in_=raw[:].rearrange("p j (a u i v) -> p u a j i v", u=2, i=2, v=2)[:, pair],
     )
 
 
@@ -64,7 +61,8 @@ def tile_moe_nxt_lin_none_kernel(
         offsets = keep.tile([P, S // LIST_ROWS], U16, name="offsets")
         token_scales = keep.tile([P, T], U8, name="token_scales", align_bytes=64)
         token_words = [keep.tile([P, T], I32, name=f"token_words{o}") for o in range(PASSES)]
-        w_raw = [keep.tile([P, PACK, N], F32, name=f"w_raw{i}", align_bytes=64) for i in range(CHUNKS)]
+        w_raw = [keep.tile([P, PACK, N], F32, name=f"w_raw{i}", align_bytes=64) for i in range(LAST)]
+        w_last = [keep.tile([P, PACK, N // 2], F32, name=f"w_last{n}", align_bytes=64) for n in range(2)]
         wp_raw = keep.tile([P, PACK, M], F32, name="wp_raw")
         gate_rows = keep.tile([P, P], F32, name="gate_rows")
         windows = [keep.tile([P, T], F32, name=f"window{r}") for r in range(ROW_GROUPS)]
@@ -93,13 +91,16 @@ def tile_moe_nxt_lin_none_kernel(
             e, o = divmod(i, PASSES)
             rows = w[e, o * P * PACK : (o + 1) * P * PACK, :]
             rows = rows.rearrange("(p j) n -> p j n", j=PACK)
-            for columns in COLUMN_HALVES if i == LAST else WHOLE:
-                nc.sync.dma_start(out=w_raw[i][:, :, columns], in_=rows[:, :, columns])
+            if i < LAST:
+                nc.sync.dma_start(out=w_raw[i][:], in_=rows)
+                return
+            for n, columns in enumerate(COLUMN_HALVES):
+                nc.sync.dma_start(out=w_last[n][:], in_=rows[:, :, columns])
 
         def load_wp():
-            rows = wp.rearrange("(a t i) f -> t a i f", t=PACK, i=RUN)
-            for t in range(PACK):
-                nc.sync.dma_start(out=wp_raw[:, t, :], in_=rows[t])
+            rows = wp.rearrange("(a u i v) f -> u a i (v f)", u=2, i=2, v=2)
+            for u in range(2):
+                nc.sync.dma_start(out=wp_raw[:, 2 * u : 2 * u + 2, :].rearrange("p v f -> p (v f)"), in_=rows[u])
 
         nc.sync.dma_start(offsets[:], offs)
         load_tokens(0)
@@ -152,19 +153,16 @@ def tile_moe_nxt_lin_none_kernel(
 
         def round_chunk(i):
             grouped = ring.tile([P, PACK, P, PACK], BF16, name="grouped", align_bytes=64)
-            every, first, second = slice(0, RUN_SETS), slice(0, RUN_SETS // 2), slice(RUN_SETS // 2, RUN_SETS)
             if i == LAST:
-                round_w(nc.vector.tensor_copy, grouped, w_raw[i], slice(0, 2), first)
-                round_w(nc.scalar.copy, grouped, w_raw[i], slice(2, 4), first)
-                round_w(nc.vector.tensor_copy, grouped, w_raw[i], slice(0, 2), second)
-                round_w(nc.vector.tensor_copy, grouped, w_raw[i], slice(2, 3), second)
-                round_w(nc.scalar.copy, grouped, w_raw[i], slice(3, 4), second)
+                for n in range(2):
+                    share = grouped[:, :, n * P // 2 : (n + 1) * P // 2]
+                    round_w(nc.vector.tensor_copy, share, w_last[n], 0)
+                    round_w(nc.scalar.copy, share, w_last[n], 1)
                 return grouped
-            split = 0 if i < PASSES else PACK - SCALAR_TILES[i % PASSES]
-            for t in range(0, split, 2):
-                round_w(nc.vector.tensor_copy, grouped, w_raw[i], slice(t, t + 2), every)
-            if split < PACK:
-                round_w(nc.scalar.copy, grouped, w_raw[i], slice(split, PACK), every)
+            split = 0 if i < PASSES else 2 - SCALAR_PAIRS[i % PASSES]
+            for pair in range(2):
+                copy = nc.vector.tensor_copy if pair < split else nc.scalar.copy
+                round_w(copy, grouped[:], w_raw[i], pair)
             return grouped
 
         def quantize_chunk(i, grouped):
@@ -174,28 +172,42 @@ def tile_moe_nxt_lin_none_kernel(
                 w_codes = ring.tile([P, N], U32, name="w_codes", align_bytes=64, bufs=4)
             w_scales = ring.tile([P, N], U8, name="w_scales", align_bytes=64, bufs=4)
             words = grouped[:].rearrange("p t m j -> p (t m) j")
-            for columns in COLUMN_HALVES if i >= PASSES else WHOLE:
+            for columns in COLUMN_HALVES:
                 values = words[:, columns, :].rearrange("p c j -> p (c j)")
                 quantize(nc, w_codes[:, columns], w_scales[:, columns], values)
             return w_codes, w_scales
 
+        def multiply(bank, t, slots, i, w_codes, w_scales, start, stop):
+            e, o = divmod(i, PASSES)
+            g, first = divmod(e * C, GATHER)
+            slots = slice(first + slots.start, first + slots.stop)
+            nc.tensor.matmul_mx(
+                out=bank,
+                lhsT=w_codes[:, t * P : (t + 1) * P].bitcast(FP8X4),
+                lhsT_scale=w_scales[:, t * P : (t + 1) * P],
+                rhs=slot_words[g, o][:, slots].bitcast(FP8X4),
+                rhs_scale=slot_scales[g][4 * o :, slots],
+                start=start,
+                stop=stop,
+            )
+
         def multiply_chunk(i, w_codes, w_scales):
             e, o = divmod(i, PASSES)
-            for pair in range(2):
+            for u in range(2):
+                if e < E - 1:
+                    if o == 0:
+                        banks[e, u] = psum.tile([P, 2, C], F32, name=f"sums{u}")
+                    for v in range(2):
+                        start, stop = (o, v) == (0, 0), (o, v) == (PASSES - 1, 1)
+                        multiply(banks[e, u][:, v, :], 2 * u + v, slice(0, C), i, w_codes, w_scales, start, stop)
+                    continue
                 for h in range(HALVES):
-                    if (o, pair) == (0, 0):
+                    if (o, u) == (0, 0):
                         banks[e, h] = psum.tile([P, PACK, P], F32, name=f"sums{h}")
-                    g, first = divmod(e * C + h * P, GATHER)
-                    for t in range(2 * pair, 2 * pair + 2):
-                        nc.tensor.matmul_mx(
-                            out=banks[e, h][:, t, :],
-                            lhsT=w_codes[:, t * P : (t + 1) * P].bitcast(FP8X4),
-                            lhsT_scale=w_scales[:, t * P : (t + 1) * P],
-                            rhs=slot_words[g, o][:, first : first + P].bitcast(FP8X4),
-                            rhs_scale=slot_scales[g][4 * o :, first : first + P],
-                            start=((o, t) == (0, 0)),
-                            stop=((o, t) == (PASSES - 1, PACK - 1)),
-                        )
+                    for t in range(2 * u, 2 * u + 2):
+                        start, stop = (o, t) == (0, 0), (o, t) == (PASSES - 1, PACK - 1)
+                        slots = slice(h * P, (h + 1) * P)
+                        multiply(banks[e, h][:, t, :], t, slots, i, w_codes, w_scales, start, stop)
 
         def project(bank, r, c_codes, c_scales):
             nc.tensor.matmul_mx(
@@ -210,12 +222,26 @@ def tile_moe_nxt_lin_none_kernel(
 
         def gate_and_project(e):
             c_grouped = keep.tile([P, HALVES, P, PACK], BF16, name="c_grouped", tag="c_bytes", align_bytes=64)
-            for h in range(HALVES):
-                factors = gates[:, e * HALVES + h, :].rearrange("p (c i) -> p c i", i=RUN)
+            if e < E - 1:
+                pairs = keep.tile([P, 2, C, 2], BF16, name="pairs")
+                factors = gates[:, e * HALVES : (e + 1) * HALVES, :].rearrange("p h (c i) -> p (h c) i", i=4)
+                for u in range(2):
+                    nc.vector.tensor_tensor(
+                        pairs[:, u].rearrange("p (c i) v -> p c v i", i=4),
+                        banks[e, u][:].rearrange("p v (c i) -> p c v i", i=4),
+                        factors.unsqueeze(2).to_broadcast([P, C // 4, 2, 4]),
+                        mybir.AluOpType.mult,
+                    )
+                nc.vector.tensor_copy(
+                    out=c_grouped[:].rearrange("p h s t -> p (h s t)").bitcast(F32).rearrange("p (s u) -> p s u", u=2),
+                    in_=pairs[:].rearrange("p u s v -> p (u s v)").bitcast(F32).rearrange("p (u s) -> p s u", u=2),
+                )
+            for h in range(HALVES if e == E - 1 else 0):
+                factors = gates[:, e * HALVES + h, :].rearrange("p (c i) -> p c i", i=2)
                 nc.vector.tensor_tensor(
-                    c_grouped[:, h].rearrange("p (c i) t -> p c t i", i=RUN),
-                    banks[e, h][:].rearrange("p t (c i) -> p c t i", i=RUN),
-                    factors.unsqueeze(2).to_broadcast([P, P // RUN, PACK, RUN]),
+                    c_grouped[:, h].rearrange("p (c i) t -> p c t i", i=2),
+                    banks[e, h][:].rearrange("p t (c i) -> p c t i", i=2),
+                    factors.unsqueeze(2).to_broadcast([P, P // 2, PACK, 2]),
                     mybir.AluOpType.mult,
                 )
             c_codes = ring.tile([P, C], U32, name="c_codes", align_bytes=64, bufs=2)
@@ -230,11 +256,12 @@ def tile_moe_nxt_lin_none_kernel(
             for h in range(HALVES):
                 slots = slice(h * P, (h + 1) * P)
                 quantize(nc, c_codes[:, slots], c_scales[:, slots], c_grouped[:, h].rearrange("p s t -> p (s t)"))
-                for r in range(ROW_GROUPS):
-                    bank = psum.tile([P, P], F32, name="spread", bufs=4)
-                    project(bank[:], r, c_codes[:, slots], c_scales[:, slots])
-                    copy = nc.vector.tensor_copy if r == 0 else nc.scalar.copy
-                    copy(out=results[r][:, slots], in_=bank[:])
+                bank = psum.tile([P, P], F32, name="spread", bufs=4)
+                project(bank[:], 0, c_codes[:, slots], c_scales[:, slots])
+                nc.vector.tensor_copy(out=results[0][:, slots], in_=bank[:])
+            bank = psum.tile([P, C], F32, name="spread", bufs=4)
+            project(bank[:], 1, c_codes[:], c_scales[:])
+            nc.scalar.copy(out=results[1][:], in_=bank[:])
             nc.vector.tensor_copy(out=windows[0][:].indirect(slot_offsets(e * C, C)), in_=results[0][:])
             nc.scalar.activation(windows[1][:].indirect(slot_offsets(e * C, C)), results[1][:], COPY)
 
@@ -257,7 +284,7 @@ def tile_moe_nxt_lin_none_kernel(
                     if (e - 1, r) != (E - 2, 1):
                         put_back(e - 1, r, w_raw[i][:, r, N - C : N])
             if i == LAST:
-                put_back(E - 2, 1, w_raw[i][:, 0, N - C : N])
+                put_back(E - 2, 1, w_last[1][:, 0, :])
             multiply_chunk(i, *quantised)
             if i == PASSES - 1:
                 interleave(nc.scalar.copy, wp_grouped, wp_raw, 0, M)

@@ -102,12 +102,12 @@ def tile_moe_nxt_lin_none_kernel(
             for u in range(2):
                 nc.sync.dma_start(out=wp_raw[:, 2 * u : 2 * u + 2, :].rearrange("p v f -> p (v f)"), in_=rows[u])
 
-        nc.sync.dma_start(offsets[:], offs)
         load_tokens(0)
+        nc.sync.dma_start(offsets[:], offs)
         load_tokens(1)
         load_token_scales()
-        load_gate()
         load_chunk(0)
+        load_gate()
         load_tokens(2)
         load_chunk(1)
         load_tokens(3)

@@ -27,14 +27,24 @@ FP8X4 = mybir.dt.float8_e4m3fn_x4
 COPY = mybir.ActivationFunctionType.Copy
 
 LAST = CHUNKS - 1
+TOKEN_LOADS = ((0, 1), (1, 1), (2, 1), (3, 1))
+W_LOADS = tuple((i, 1) for i in range(LAST))
 COLUMN_HALVES = (slice(0, N // 2), slice(N // 2, N))
 SCALAR_PAIRS = (2, 1, 0, 0)
+FIRST_PAIRS = (2, 2, 2, 2)
 
 
 def round_w(copy, grouped, raw, pair):
     copy(
         out=grouped.rearrange("p (u v) (a i) j -> p u a j i v", v=2, i=2)[:, pair],
         in_=raw[:].rearrange("p j (a u i v) -> p u a j i v", u=2, i=2, v=2)[:, pair],
+    )
+
+
+def round_tile(copy, grouped, raw, t):
+    copy(
+        out=grouped[:, t].rearrange("p (a i) j -> p a j i", i=2),
+        in_=raw[:].rearrange("p j (a u i v) -> p u v a j i", u=2, i=2, v=2)[:, t // 2, t % 2],
     )
 
 
@@ -60,8 +70,14 @@ def tile_moe_nxt_lin_none_kernel(
 
         offsets = keep.tile([P, S // LIST_ROWS], U16, name="offsets")
         token_scales = keep.tile([P, T], U8, name="token_scales", align_bytes=64)
-        token_words = [keep.tile([P, T], I32, name=f"token_words{o}") for o in range(PASSES)]
-        w_raw = [keep.tile([P, PACK, N], F32, name=f"w_raw{i}", align_bytes=64) for i in range(LAST)]
+        token_loads = {
+            first: keep.tile([P, count, T], I32, name=f"token_words{first}") for first, count in TOKEN_LOADS
+        }
+        token_words = [token_loads[first][:, o, :] for first, count in TOKEN_LOADS for o in range(count)]
+        w_loads = {
+            first: keep.tile([P, count, PACK, N], F32, name=f"w_raw{first}", align_bytes=64) for first, count in W_LOADS
+        }
+        w_raw = [w_loads[first][:, i] for first, count in W_LOADS for i in range(count)]
         w_last = [keep.tile([P, PACK, N // 2], F32, name=f"w_last{n}", align_bytes=64) for n in range(2)]
         wp_raw = keep.tile([P, PACK, M], F32, name="wp_raw")
         gate_rows = keep.tile([P, P], F32, name="gate_rows")
@@ -73,8 +89,10 @@ def tile_moe_nxt_lin_none_kernel(
         make_identity(nc, identity[:])
 
         def load_tokens(o):
-            words = x_words[o].rearrange("p t r -> p (t r)").bitcast(I32)
-            nc.sync.dma_start(out=token_words[o][:], in_=words)
+            if o in token_loads:
+                count = token_loads[o].shape[1]
+                words = x_words[o : o + count].rearrange("o p t r -> p o (t r)").bitcast(I32)
+                nc.sync.dma_start(out=token_loads[o][:], in_=words)
 
         def load_token_scales():
             for quadrant in range(4):
@@ -92,7 +110,11 @@ def tile_moe_nxt_lin_none_kernel(
             rows = w[e, o * P * PACK : (o + 1) * P * PACK, :]
             rows = rows.rearrange("(p j) n -> p j n", j=PACK)
             if i < LAST:
-                nc.sync.dma_start(out=w_raw[i][:], in_=rows)
+                if i in w_loads:
+                    count = w_loads[i].shape[1]
+                    rows = w[e, o * P * PACK : (o + count) * P * PACK, :]
+                    rows = rows.rearrange("(c p j) n -> p c (j n)", c=count, j=PACK)
+                    nc.sync.dma_start(out=w_loads[i][:].rearrange("p c j n -> p c (j n)"), in_=rows)
                 return
             for n, columns in enumerate(COLUMN_HALVES):
                 nc.sync.dma_start(out=w_last[n][:], in_=rows[:, :, columns])
@@ -159,22 +181,33 @@ def tile_moe_nxt_lin_none_kernel(
                     round_w(nc.vector.tensor_copy, share, w_last[n], 0)
                     round_w(nc.scalar.copy, share, w_last[n], 1)
                 return grouped
-            split = 0 if i < PASSES else 2 - SCALAR_PAIRS[i % PASSES]
+            if i >= PASSES and i % PASSES == 0:
+                round_tile(nc.scalar.copy, grouped, w_raw[i], 0)
+                round_tile(nc.vector.tensor_copy, grouped, w_raw[i], 1)
+                round_w(nc.scalar.copy, grouped[:], w_raw[i], 1)
+                return grouped
+            split = 2 - (FIRST_PAIRS if i < PASSES else SCALAR_PAIRS)[i % PASSES]
             for pair in range(2):
                 copy = nc.vector.tensor_copy if pair < split else nc.scalar.copy
                 round_w(copy, grouped[:], w_raw[i], pair)
             return grouped
 
         def quantize_chunk(i, grouped):
-            if i >= PASSES and i % PASSES == 0:
-                w_codes = keep.tile([P, N], U32, name="codes_after_c", tag="c_bytes", align_bytes=64)
-            else:
-                w_codes = ring.tile([P, N], U32, name="w_codes", align_bytes=64, bufs=4)
+            w_codes = {}
             w_scales = ring.tile([P, N], U8, name="w_scales", align_bytes=64, bufs=4)
             words = grouped[:].rearrange("p t m j -> p (t m) j")
-            for columns in COLUMN_HALVES:
-                values = words[:, columns, :].rearrange("p c j -> p (c j)")
-                quantize(nc, w_codes[:, columns], w_scales[:, columns], values)
+            for u in range(2):
+                columns = COLUMN_HALVES[u]
+                if i >= PASSES and i % PASSES == 0 and u == 1:
+                    codes = keep.tile([P, N // 2], U32, name="codes_after_c", tag="c_bytes", align_bytes=64)
+                else:
+                    codes = ring.tile([P, N // 2], U32, name="w_codes", align_bytes=64, bufs=8)
+                width = P if i >= PASSES and i % PASSES == 0 and u == 0 else N // 2
+                for first in range(0, N // 2, width):
+                    part = slice(columns.start + first, columns.start + first + width)
+                    values = words[:, part, :].rearrange("p c j -> p (c j)")
+                    quantize(nc, codes[:, first : first + width], w_scales[:, part], values)
+                w_codes[u] = codes
             return w_codes, w_scales
 
         def multiply(bank, t, slots, i, w_codes, w_scales, start, stop):
@@ -183,7 +216,7 @@ def tile_moe_nxt_lin_none_kernel(
             slots = slice(first + slots.start, first + slots.stop)
             nc.tensor.matmul_mx(
                 out=bank,
-                lhsT=w_codes[:, t * P : (t + 1) * P].bitcast(FP8X4),
+                lhsT=w_codes[t // 2][:, t % 2 * P : (t % 2 + 1) * P].bitcast(FP8X4),
                 lhsT_scale=w_scales[:, t * P : (t + 1) * P],
                 rhs=slot_words[g, o][:, slots].bitcast(FP8X4),
                 rhs_scale=slot_scales[g][4 * o :, slots],
@@ -200,14 +233,13 @@ def tile_moe_nxt_lin_none_kernel(
                     for v in range(2):
                         start, stop = (o, v) == (0, 0), (o, v) == (PASSES - 1, 1)
                         multiply(banks[e, u][:, v, :], 2 * u + v, slice(0, C), i, w_codes, w_scales, start, stop)
-                    continue
-                for h in range(HALVES):
-                    if (o, u) == (0, 0):
-                        banks[e, h] = psum.tile([P, PACK, P], F32, name=f"sums{h}")
-                    for t in range(2 * u, 2 * u + 2):
-                        start, stop = (o, t) == (0, 0), (o, t) == (PASSES - 1, PACK - 1)
-                        slots = slice(h * P, (h + 1) * P)
-                        multiply(banks[e, h][:, t, :], t, slots, i, w_codes, w_scales, start, stop)
+            for h in range(HALVES if e == E - 1 else 0):
+                if o == 0:
+                    banks[e, h] = psum.tile([P, PACK, P], F32, name=f"sums{h}")
+                tiles = (3, 0, 1, 2) if (o, h) == (PASSES - 1, 1) else (0, 1, 2, 3)
+                for t in tiles:
+                    start, stop = (o, t) == (0, tiles[0]), (o, t) == (PASSES - 1, tiles[-1])
+                    multiply(banks[e, h][:, t, :], t, slice(h * P, (h + 1) * P), i, w_codes, w_scales, start, stop)
 
         def project(bank, r, c_codes, c_scales):
             nc.tensor.matmul_mx(

@@ -31,6 +31,7 @@ TOKEN_LOADS = ((0, 1), (1, 1), (2, 1), (3, 1))
 W_LOADS = tuple((i, 1) for i in range(LAST))
 COLUMN_HALVES = (slice(0, N // 2), slice(N // 2, N))
 SCALAR_PAIRS = (2, 1, 0, 0)
+LAST_PARTS = ((0, slice(0, P)), (1, slice(0, P // 2)), (1, slice(P // 2, P)))
 FIRST_PAIRS = (2, 2, 2, 2)
 
 
@@ -178,8 +179,12 @@ def tile_moe_nxt_lin_none_kernel(
             if i == LAST:
                 for n in range(2):
                     share = grouped[:, :, n * P // 2 : (n + 1) * P // 2]
-                    round_w(nc.vector.tensor_copy, share, w_last[n], 0)
-                    round_w(nc.scalar.copy, share, w_last[n], 1)
+                    if n == 0:
+                        round_w(nc.vector.tensor_copy, share, w_last[n], 0)
+                        round_w(nc.scalar.copy, share, w_last[n], 1)
+                    else:
+                        for t in range(PACK):
+                            round_tile(nc.vector.tensor_copy if t < 2 else nc.scalar.copy, share, w_last[n], t)
                 return grouped
             if i >= PASSES and i % PASSES == 0:
                 round_tile(nc.scalar.copy, grouped, w_raw[i], 0)
@@ -202,7 +207,7 @@ def tile_moe_nxt_lin_none_kernel(
                     codes = keep.tile([P, N // 2], U32, name="codes_after_c", tag="c_bytes", align_bytes=64)
                 else:
                     codes = ring.tile([P, N // 2], U32, name="w_codes", align_bytes=64, bufs=8)
-                width = P if i >= PASSES and i % PASSES == 0 and u == 0 else N // 2
+                width = P if i == LAST or (i >= PASSES and i % PASSES == 0 and u == 0) else N // 2
                 for first in range(0, N // 2, width):
                     part = slice(columns.start + first, columns.start + first + width)
                     values = words[:, part, :].rearrange("p c j -> p (c j)")
@@ -268,12 +273,12 @@ def tile_moe_nxt_lin_none_kernel(
                     out=c_grouped[:].rearrange("p h s t -> p (h s t)").bitcast(F32).rearrange("p (s u) -> p s u", u=2),
                     in_=pairs[:].rearrange("p u s v -> p (u s v)").bitcast(F32).rearrange("p (u s) -> p s u", u=2),
                 )
-            for h in range(HALVES if e == E - 1 else 0):
-                factors = gates[:, e * HALVES + h, :].rearrange("p (c i) -> p c i", i=2)
+            for h, part in LAST_PARTS if e == E - 1 else ():
+                factors = gates[:, e * HALVES + h, part].rearrange("p (c i) -> p c i", i=2)
                 nc.vector.tensor_tensor(
-                    c_grouped[:, h].rearrange("p (c i) t -> p c t i", i=2),
-                    banks[e, h][:].rearrange("p t (c i) -> p c t i", i=2),
-                    factors.unsqueeze(2).to_broadcast([P, P // 2, PACK, 2]),
+                    c_grouped[:, h, part].rearrange("p (c i) t -> p c t i", i=2),
+                    banks[e, h][:, :, part].rearrange("p t (c i) -> p c t i", i=2),
+                    factors.unsqueeze(2).to_broadcast([P, (part.stop - part.start) // 2, PACK, 2]),
                     mybir.AluOpType.mult,
                 )
             c_codes = ring.tile([P, C], U32, name="c_codes", align_bytes=64, bufs=2)
@@ -285,10 +290,11 @@ def tile_moe_nxt_lin_none_kernel(
                     project(projected[e, r][:], r, c_codes[:], c_scales[:])
                 return
             results = [keep.tile([P, C], F32, name=f"last_results{r}") for r in range(ROW_GROUPS)]
-            for h in range(HALVES):
-                slots = slice(h * P, (h + 1) * P)
-                quantize(nc, c_codes[:, slots], c_scales[:, slots], c_grouped[:, h].rearrange("p s t -> p (s t)"))
-                bank = psum.tile([P, P], F32, name="spread", bufs=4)
+            for h, part in LAST_PARTS:
+                slots = slice(h * P + part.start, h * P + part.stop)
+                values = c_grouped[:, h, part].rearrange("p s t -> p (s t)")
+                quantize(nc, c_codes[:, slots], c_scales[:, slots], values)
+                bank = psum.tile([P, part.stop - part.start], F32, name="spread", bufs=4)
                 project(bank[:], 0, c_codes[:, slots], c_scales[:, slots])
                 nc.vector.tensor_copy(out=results[0][:, slots], in_=bank[:])
             bank = psum.tile([P, C], F32, name="spread", bufs=4)

@@ -32,20 +32,20 @@ W_LOADS = tuple((i, 1) for i in range(LAST))
 COLUMN_HALVES = (slice(0, N // 2), slice(N // 2, N))
 SCALAR_PAIRS = (2, 1, 0, 0)
 LAST_PARTS = ((0, slice(0, P)), (1, slice(0, P // 2)), (1, slice(P // 2, P)))
-FIRST_PAIRS = (2, 2, 2, 2)
+FIRST_PAIRS = (2, 2, 2, 1)
 
 
 def round_w(copy, grouped, raw, pair):
     copy(
-        out=grouped.rearrange("p (u v) (a i) j -> p u a j i v", v=2, i=2)[:, pair],
-        in_=raw[:].rearrange("p j (a u i v) -> p u a j i v", u=2, i=2, v=2)[:, pair],
+        out=grouped.rearrange("p (u v) (a i) j -> p u a j v i", v=2, i=2)[:, pair],
+        in_=raw[:].rearrange("p j (a u v i) -> p u a j v i", u=2, i=2, v=2)[:, pair],
     )
 
 
 def round_tile(copy, grouped, raw, t):
     copy(
         out=grouped[:, t].rearrange("p (a i) j -> p a j i", i=2),
-        in_=raw[:].rearrange("p j (a u i v) -> p u v a j i", u=2, i=2, v=2)[:, t // 2, t % 2],
+        in_=raw[:].rearrange("p j (a u v i) -> p u v a j i", u=2, i=2, v=2)[:, t // 2, t % 2],
     )
 
 
@@ -121,9 +121,9 @@ def tile_moe_nxt_lin_none_kernel(
                 nc.sync.dma_start(out=w_last[n][:], in_=rows[:, :, columns])
 
         def load_wp():
-            rows = wp.rearrange("(a u i v) f -> u a i (v f)", u=2, i=2, v=2)
-            for u in range(2):
-                nc.sync.dma_start(out=wp_raw[:, 2 * u : 2 * u + 2, :].rearrange("p v f -> p (v f)"), in_=rows[u])
+            rows = wp.rearrange("(a t i) f -> i a t f", t=PACK, i=2)
+            for i in range(2):
+                nc.sync.dma_start(out=wp_raw[i:P:2], in_=rows[i])
 
         load_tokens(0)
         nc.sync.dma_start(offsets[:], offs)
@@ -131,12 +131,12 @@ def tile_moe_nxt_lin_none_kernel(
         load_token_scales()
         load_chunk(0)
         load_gate()
+        load_wp()
         load_tokens(2)
         load_chunk(1)
         load_tokens(3)
         load_chunk(2)
         load_chunk(3)
-        load_wp()
         for i in range(PASSES, CHUNKS):
             load_chunk(i)
 
@@ -324,7 +324,7 @@ def tile_moe_nxt_lin_none_kernel(
             if i == LAST:
                 put_back(E - 2, 1, w_last[1][:, 0, :])
             multiply_chunk(i, *quantised)
-            if i == PASSES - 1:
+            if i == 0:
                 interleave(nc.scalar.copy, wp_grouped, wp_raw, 0, M)
                 quantize(nc, wp_codes[:], wp_scales[:], wp_grouped[:].rearrange("p c j -> p (c j)"))
             if o == PASSES - 1:

@@ -31,6 +31,7 @@ TOKEN_LOADS = ((0, 1), (1, 1), (2, 1), (3, 1))
 W_LOADS = tuple((i, 1) for i in range(LAST))
 COLUMN_HALVES = (slice(0, N // 2), slice(N // 2, N))
 SCALAR_PAIRS = (2, 1, 0, 0)
+LAST_LOADS = (slice(0, N // 2), slice(N // 2, 3 * N // 4), slice(3 * N // 4, N))
 LAST_PARTS = ((0, slice(0, P)), (1, slice(0, P // 2)), (1, slice(P // 2, P)))
 FIRST_PAIRS = (2, 2, 2, 1)
 
@@ -79,7 +80,10 @@ def tile_moe_nxt_lin_none_kernel(
             first: keep.tile([P, count, PACK, N], F32, name=f"w_raw{first}", align_bytes=64) for first, count in W_LOADS
         }
         w_raw = [w_loads[first][:, i] for first, count in W_LOADS for i in range(count)]
-        w_last = [keep.tile([P, PACK, N // 2], F32, name=f"w_last{n}", align_bytes=64) for n in range(2)]
+        w_last = [
+            keep.tile([P, PACK, columns.stop - columns.start], F32, name=f"w_last{n}", align_bytes=64)
+            for n, columns in enumerate(LAST_LOADS)
+        ]
         wp_raw = keep.tile([P, PACK, M], F32, name="wp_raw")
         gate_rows = keep.tile([P, P], F32, name="gate_rows")
         windows = [keep.tile([P, T], F32, name=f"window{r}") for r in range(ROW_GROUPS)]
@@ -117,7 +121,7 @@ def tile_moe_nxt_lin_none_kernel(
                     rows = rows.rearrange("(c p j) n -> p c (j n)", c=count, j=PACK)
                     nc.sync.dma_start(out=w_loads[i][:].rearrange("p c j n -> p c (j n)"), in_=rows)
                 return
-            for n, columns in enumerate(COLUMN_HALVES):
+            for n, columns in enumerate(LAST_LOADS):
                 nc.sync.dma_start(out=w_last[n][:], in_=rows[:, :, columns])
 
         def load_wp():
@@ -177,9 +181,9 @@ def tile_moe_nxt_lin_none_kernel(
         def round_chunk(i):
             grouped = ring.tile([P, PACK, P, PACK], BF16, name="grouped", align_bytes=64)
             if i == LAST:
-                for n in range(2):
-                    share = grouped[:, :, n * P // 2 : (n + 1) * P // 2]
-                    if n == 0:
+                for n, columns in enumerate(LAST_LOADS):
+                    share = grouped[:, :, columns.start // PACK : columns.stop // PACK]
+                    if n < len(LAST_LOADS) - 1:
                         round_w(nc.vector.tensor_copy, share, w_last[n], 0)
                         round_w(nc.scalar.copy, share, w_last[n], 1)
                     else:
@@ -191,6 +195,15 @@ def tile_moe_nxt_lin_none_kernel(
                 round_tile(nc.vector.tensor_copy, grouped, w_raw[i], 1)
                 round_w(nc.scalar.copy, grouped[:], w_raw[i], 1)
                 return grouped
+            if i == LAST - 2:
+                for pair in range(2):
+                    round_w(nc.vector.tensor_copy, grouped[:], w_raw[i], pair)
+                return grouped
+            if i == LAST - 1:
+                round_w(nc.vector.tensor_copy, grouped[:], w_raw[i], 0)
+                round_tile(nc.vector.tensor_copy, grouped, w_raw[i], 2)
+                round_tile(nc.scalar.copy, grouped, w_raw[i], 3)
+                return grouped
             split = 2 - (FIRST_PAIRS if i < PASSES else SCALAR_PAIRS)[i % PASSES]
             for pair in range(2):
                 copy = nc.vector.tensor_copy if pair < split else nc.scalar.copy
@@ -201,13 +214,23 @@ def tile_moe_nxt_lin_none_kernel(
             w_codes = {}
             w_scales = ring.tile([P, N], U8, name="w_scales", align_bytes=64, bufs=4)
             words = grouped[:].rearrange("p t m j -> p (t m) j")
+            if i == LAST:
+                for u in range(2):
+                    w_codes[u] = ring.tile([P, N // 2], U32, name="w_codes", align_bytes=64, bufs=8)
+                for first in range(0, P, P // 2):
+                    for t in range(PACK):
+                        part = slice(t * P + first, t * P + first + P // 2)
+                        values = words[:, part, :].rearrange("p c j -> p (c j)")
+                        codes = w_codes[t // 2][:, t % 2 * P + first : t % 2 * P + first + P // 2]
+                        quantize(nc, codes, w_scales[:, part], values)
+                return w_codes, w_scales
             for u in range(2):
                 columns = COLUMN_HALVES[u]
                 if i >= PASSES and i % PASSES == 0 and u == 1:
                     codes = keep.tile([P, N // 2], U32, name="codes_after_c", tag="c_bytes", align_bytes=64)
                 else:
                     codes = ring.tile([P, N // 2], U32, name="w_codes", align_bytes=64, bufs=8)
-                width = P if i == LAST or (i >= PASSES and i % PASSES == 0 and u == 0) else N // 2
+                width = P if i >= PASSES and i % PASSES == 0 and u == 0 else N // 2
                 for first in range(0, N // 2, width):
                     part = slice(columns.start + first, columns.start + first + width)
                     values = words[:, part, :].rearrange("p c j -> p (c j)")
@@ -232,16 +255,16 @@ def tile_moe_nxt_lin_none_kernel(
         def multiply_chunk(i, w_codes, w_scales):
             e, o = divmod(i, PASSES)
             for u in range(2):
-                if e < E - 1:
+                if e < E - 2:
                     if o == 0:
                         banks[e, u] = psum.tile([P, 2, C], F32, name=f"sums{u}")
                     for v in range(2):
                         start, stop = (o, v) == (0, 0), (o, v) == (PASSES - 1, 1)
                         multiply(banks[e, u][:, v, :], 2 * u + v, slice(0, C), i, w_codes, w_scales, start, stop)
-            for h in range(HALVES if e == E - 1 else 0):
+            for h in range(HALVES if e >= E - 2 else 0):
                 if o == 0:
                     banks[e, h] = psum.tile([P, PACK, P], F32, name=f"sums{h}")
-                tiles = (3, 0, 1, 2) if (o, h) == (PASSES - 1, 1) else (0, 1, 2, 3)
+                tiles = (3, 0, 1, 2) if (i, h) == (LAST, 1) else (0, 1, 2, 3)
                 for t in tiles:
                     start, stop = (o, t) == (0, tiles[0]), (o, t) == (PASSES - 1, tiles[-1])
                     multiply(banks[e, h][:, t, :], t, slice(h * P, (h + 1) * P), i, w_codes, w_scales, start, stop)
@@ -259,7 +282,7 @@ def tile_moe_nxt_lin_none_kernel(
 
         def gate_and_project(e):
             c_grouped = keep.tile([P, HALVES, P, PACK], BF16, name="c_grouped", tag="c_bytes", align_bytes=64)
-            if e < E - 1:
+            if e < E - 2:
                 pairs = keep.tile([P, 2, C, 2], BF16, name="pairs")
                 factors = gates[:, e * HALVES : (e + 1) * HALVES, :].rearrange("p h (c i) -> p (h c) i", i=4)
                 for u in range(2):
@@ -273,7 +296,7 @@ def tile_moe_nxt_lin_none_kernel(
                     out=c_grouped[:].rearrange("p h s t -> p (h s t)").bitcast(F32).rearrange("p (s u) -> p s u", u=2),
                     in_=pairs[:].rearrange("p u s v -> p (u s v)").bitcast(F32).rearrange("p (u s) -> p s u", u=2),
                 )
-            for h, part in LAST_PARTS if e == E - 1 else ():
+            for h, part in (((), (), ((0, slice(0, P)), (1, slice(0, P))), LAST_PARTS)[e]):
                 factors = gates[:, e * HALVES + h, part].rearrange("p (c i) -> p c i", i=2)
                 nc.vector.tensor_tensor(
                     c_grouped[:, h, part].rearrange("p (c i) t -> p c t i", i=2),
@@ -284,7 +307,11 @@ def tile_moe_nxt_lin_none_kernel(
             c_codes = ring.tile([P, C], U32, name="c_codes", align_bytes=64, bufs=2)
             c_scales = ring.tile([P, C], U8, name="c_scales", align_bytes=64, bufs=2)
             if e < E - 1:
-                quantize(nc, c_codes[:], c_scales[:], c_grouped[:].rearrange("p h s t -> p (h s t)"))
+                for h in range(0, HALVES, HALVES if e < E - 2 else 1):
+                    count = HALVES if e < E - 2 else 1
+                    slots = slice(h * P, (h + count) * P)
+                    values = c_grouped[:, h : h + count].rearrange("p h s t -> p (h s t)")
+                    quantize(nc, c_codes[:, slots], c_scales[:, slots], values)
                 for r in range(ROW_GROUPS):
                     projected[e, r] = psum.tile([P, C], F32, name="spread", bufs=4)
                     project(projected[e, r][:], r, c_codes[:], c_scales[:])
@@ -303,8 +330,7 @@ def tile_moe_nxt_lin_none_kernel(
             nc.vector.tensor_copy(out=windows[0][:].indirect(slot_offsets(e * C, C)), in_=results[0][:])
             nc.scalar.activation(windows[1][:].indirect(slot_offsets(e * C, C)), results[1][:], COPY)
 
-        def put_back(e, r, results):
-            nc.scalar.copy(out=results, in_=projected[e, r][:])
+        def scatter(e, r, results):
             nc.scalar.activation(windows[r][:].indirect(slot_offsets(e * C, C)), results, COPY)
 
         for g in range(S // GATHER):
@@ -318,11 +344,16 @@ def tile_moe_nxt_lin_none_kernel(
             if i < PASSES:
                 gather_words(1, i)
             if e > 0 and o == 1:
-                for r in range(ROW_GROUPS):
-                    if (e - 1, r) != (E - 2, 1):
-                        put_back(e - 1, r, w_raw[i][:, r, N - C : N])
+                groups = range(ROW_GROUPS if e < E - 1 else 1)
+                spent = w_raw[i if e < E - 1 else i - 1]
+                for r in groups:
+                    nc.scalar.copy(out=spent[:, r, N - C : N], in_=projected[e - 1, r][:])
+                for r in groups:
+                    scatter(e - 1, r, spent[:, r, N - C : N])
             if i == LAST:
-                put_back(E - 2, 1, w_last[1][:, 0, :])
+                held = w_last[-1][:, 0:2, :].rearrange("p j n -> p (j n)")
+                nc.scalar.copy(out=held, in_=projected[E - 2, 1][:])
+                scatter(E - 2, 1, held)
             multiply_chunk(i, *quantised)
             if i == 0:
                 interleave(nc.scalar.copy, wp_grouped, wp_raw, 0, M)

from contextlib import ExitStack

import concourse.mybir as mybir
from concourse.masks import make_identity

K, T, E, C, N, M = 2048, 1280, 4, 256, 512, 256
S = E * C
P = 128
PACK = 4
PASSES = K // (P * PACK)
CHUNKS = E * PASSES
HALVES = C // P
ROW_GROUPS = M // P
GATHER = 512
LIST_ROWS = 16

FLOPS = 2 * K * N * S + 2 * N * M * T
BYTES = 4 * E * K * N + K * T + K * T // 32 + 4 * N * M + 4 * S + 2 * P * S // LIST_ROWS + 4 * M * T

F32 = mybir.dt.float32
BF16 = mybir.dt.bfloat16
I32 = mybir.dt.int32
U32 = mybir.dt.uint32
U16 = mybir.dt.uint16
U8 = mybir.dt.uint8
FP8X4 = mybir.dt.float8_e4m3fn_x4
COPY = mybir.ActivationFunctionType.Copy

LAST = CHUNKS - 1
TOKEN_LOADS = ((0, 1), (1, 1), (2, 1), (3, 1))
W_LOADS = tuple((i, 1) for i in range(LAST))
COLUMN_HALVES = (slice(0, N // 2), slice(N // 2, N))
SCALAR_PAIRS = (2, 1, 0, 0)
LAST_LOADS = (slice(0, N // 2), slice(N // 2, 3 * N // 4), slice(3 * N // 4, N))
LAST_PARTS = ((0, slice(0, P)), (1, slice(0, P // 2)), (1, slice(P // 2, P)))
FIRST_PAIRS = (2, 2, 2, 1)


def round_w(copy, grouped, raw, pair):
    copy(
        out=grouped.rearrange("p (u v) (a i) j -> p u a j v i", v=2, i=2)[:, pair],
        in_=raw[:].rearrange("p j (a u v i) -> p u a j v i", u=2, i=2, v=2)[:, pair],
    )


def round_tile(copy, grouped, raw, t):
    copy(
        out=grouped[:, t].rearrange("p (a i) j -> p a j i", i=2),
        in_=raw[:].rearrange("p j (a u v i) -> p u v a j i", u=2, i=2, v=2)[:, t // 2, t % 2],
    )


def interleave(copy, grouped, raw, first, last):
    copy(
        out=grouped[:, first:last, :].rearrange("p (c i) j -> p c j i", i=4),
        in_=raw[:, :, first:last].rearrange("p j (c i) -> p c j i", i=4),
    )


def quantize(nc, codes, scales, grouped):
    nc.vector.quantize_mx(out=codes.bitcast(FP8X4), scales=scales, in_=grouped)


def tile_moe_nxt_lin_none_kernel(
    tc, x_words, x_scales, w, wp, gate, offs, out
):
    nc = tc.nc
    with ExitStack() as ctx:
        keep = ctx.enter_context(tc.tile_pool(name="keep", bufs=1))
        ring = ctx.enter_context(tc.tile_pool(name="ring", bufs=3))
        psum = ctx.enter_context(tc.psum_pool(name="psum", bufs=2))

        offsets = keep.tile([P, S // LIST_ROWS], U16, name="offsets")
        token_scales = keep.tile([P, T], U8, name="token_scales", align_bytes=64)
        token_loads = {
            first: keep.tile([P, count, T], I32, name=f"token_words{first}") for first, count in TOKEN_LOADS
        }
        token_words = [token_loads[first][:, o, :] for first, count in TOKEN_LOADS for o in range(count)]
        w_loads = {
            first: keep.tile([P, count, PACK, N], F32, name=f"w_raw{first}", align_bytes=64) for first, count in W_LOADS
        }
        w_raw = [w_loads[first][:, i] for first, count in W_LOADS for i in range(count)]
        w_last = [
            keep.tile([P, PACK, columns.stop - columns.start], F32, name=f"w_last{n}", align_bytes=64)
            for n, columns in enumerate(LAST_LOADS)
        ]
        wp_raw = keep.tile([P, PACK, M], F32, name="wp_raw")
        gate_rows = keep.tile([P, P], F32, name="gate_rows")
        windows = [keep.tile([P, T], F32, name=f"window{r}") for r in range(ROW_GROUPS)]
        identity = keep.tile([P, P], F32, name="identity")

        nc.vector.memset(token_scales[:].bitcast(I32), 0)
        nc.vector.memset(gate_rows[:], 0.0)
        make_identity(nc, identity[:])

        def load_tokens(o):
            if o in token_loads:
                count = token_loads[o].shape[1]
                words = x_words[o : o + count].rearrange("o p t r -> p o (t r)").bitcast(I32)
                nc.sync.dma_start(out=token_loads[o][:], in_=words)

        def load_token_scales():
            for quadrant in range(4):
                nc.sync.dma_start(
                    out=token_scales[32 * quadrant : 32 * quadrant + 16, :].bitcast(I32),
                    in_=x_scales[:, 4 * quadrant : 4 * quadrant + 4, :].bitcast(I32),
                )

        def load_gate():
            row = gate[0:1, :].rearrange("a (j c) -> (a j) c", c=P)
            nc.sync.dma_start(out=gate_rows[0 : S // P, :], in_=row)

        def load_chunk(i):
            e, o = divmod(i, PASSES)
            rows = w[e, o * P * PACK : (o + 1) * P * PACK, :]
            rows = rows.rearrange("(p j) n -> p j n", j=PACK)
            if i < LAST:
                if i in w_loads:
                    count = w_loads[i].shape[1]
                    rows = w[e, o * P * PACK : (o + count) * P * PACK, :]
                    rows = rows.rearrange("(c p j) n -> p c (j n)", c=count, j=PACK)
                    nc.sync.dma_start(out=w_loads[i][:].rearrange("p c j n -> p c (j n)"), in_=rows)
                return
            for n, columns in enumerate(LAST_LOADS):
                nc.sync.dma_start(out=w_last[n][:], in_=rows[:, :, columns])

        def load_wp():
            rows = wp.rearrange("(a t i) f -> i a t f", t=PACK, i=2)
            for i in range(2):
                nc.sync.dma_start(out=wp_raw[i:P:2], in_=rows[i])

        load_tokens(0)
        nc.sync.dma_start(offsets[:], offs)
        load_tokens(1)
        load_token_scales()
        load_chunk(0)
        load_gate()
        load_wp()
        load_tokens(2)
        load_chunk(1)
        load_tokens(3)
        load_chunk(2)
        load_chunk(3)
        for i in range(PASSES, CHUNKS):
            load_chunk(i)

        for r in range(ROW_GROUPS):
            nc.gpsimd.memset(windows[r][:], 0.0)

        gate_bank = psum.tile([P, PACK, P], F32, name="spread", bufs=4)
        nc.tensor.transpose(gate_bank[:, 0, :], gate_rows[:], identity[:])
        gate_columns = keep.tile([P, S // P], F32, name="gate_columns")
        nc.scalar.copy(out=gate_columns[:], in_=gate_bank[:, 0, 0 : S // P])
        gates = keep.tile([P, S // P, P], F32, name="gates")
        for first in range(0, S // P, PACK):
            spread = psum.tile([P, PACK, P], F32, name="spread", bufs=4)
            for j in range(PACK):
                column = gate_columns[:, first + j : first + j + 1].to_broadcast([P, P])
                nc.tensor.transpose(spread[:, j, :], column, identity[:])
            nc.scalar.copy(out=gates[:, first : first + PACK, :], in_=spread[:])

        wp_grouped = keep.tile([P, M, PACK], BF16, name="wp_grouped", align_bytes=64)
        wp_codes = keep.tile([P, M], U32, name="wp_codes", align_bytes=64)
        wp_scales = keep.tile([P, M], U8, name="wp_scales", align_bytes=64)

        slot_scales, slot_words, banks, projected = {}, {}, {}, {}

        def slot_offsets(first, count):
            return offsets[:, first // LIST_ROWS : (first + count) // LIST_ROWS]

        def gather_scales(g):
            slot_scales[g] = keep.tile([P, GATHER], U8, name=f"slot_scales{g}", align_bytes=64)
            window = token_scales[:].indirect(slot_offsets(g * GATHER, GATHER))
            nc.vector.tensor_copy(out=slot_scales[g][:], in_=window)

        def gather_words(g, o):
            slot_words[g, o] = keep.tile([P, GATHER], U32, name=f"slot_words{g}_{o}", align_bytes=64)
            window = token_words[o][:].bitcast(U32).indirect(slot_offsets(g * GATHER, GATHER))
            nc.vector.tensor_copy(out=slot_words[g, o][:], in_=window)

        def round_chunk(i):
            grouped = ring.tile([P, PACK, P, PACK], BF16, name="grouped", align_bytes=64)
            if i == LAST:
                for n, columns in enumerate(LAST_LOADS):
                    share = grouped[:, :, columns.start // PACK : columns.stop // PACK]
                    if n < len(LAST_LOADS) - 1:
                        round_w(nc.vector.tensor_copy, share, w_last[n], 0)
                        round_w(nc.scalar.copy, share, w_last[n], 1)
                    else:
                        for t in range(PACK):
                            round_tile(nc.vector.tensor_copy if t < 2 else nc.scalar.copy, share, w_last[n], t)
                return grouped
            if i >= PASSES and i % PASSES == 0:
                round_tile(nc.scalar.copy, grouped, w_raw[i], 0)
                round_tile(nc.vector.tensor_copy, grouped, w_raw[i], 1)
                round_w(nc.scalar.copy, grouped[:], w_raw[i], 1)
                return grouped
            if i == LAST - 2:
                for pair in range(2):
                    round_w(nc.vector.tensor_copy, grouped[:], w_raw[i], pair)
                return grouped
            if i == LAST - 1:
                round_w(nc.vector.tensor_copy, grouped[:], w_raw[i], 0)
                round_tile(nc.vector.tensor_copy, grouped, w_raw[i], 2)
                round_tile(nc.scalar.copy, grouped, w_raw[i], 3)
                return grouped
            split = 2 - (FIRST_PAIRS if i < PASSES else SCALAR_PAIRS)[i % PASSES]
            for pair in range(2):
                copy = nc.vector.tensor_copy if pair < split else nc.scalar.copy
                round_w(copy, grouped[:], w_raw[i], pair)
            return grouped

        def quantize_chunk(i, grouped):
            w_codes = {}
            w_scales = ring.tile([P, N], U8, name="w_scales", align_bytes=64, bufs=4)
            words = grouped[:].rearrange("p t m j -> p (t m) j")
            if i == LAST:
                for u in range(2):
                    w_codes[u] = ring.tile([P, N // 2], U32, name="w_codes", align_bytes=64, bufs=8)
                for first in range(0, P, P // 2):
                    for t in range(PACK):
                        part = slice(t * P + first, t * P + first + P // 2)
                        values = words[:, part, :].rearrange("p c j -> p (c j)")
                        codes = w_codes[t // 2][:, t % 2 * P + first : t % 2 * P + first + P // 2]
                        quantize(nc, codes, w_scales[:, part], values)
                return w_codes, w_scales
            for u in range(2):
                columns = COLUMN_HALVES[u]
                if i >= PASSES and i % PASSES == 0 and u == 1:
                    codes = keep.tile([P, N // 2], U32, name="codes_after_c", tag="c_bytes", align_bytes=64)
                else:
                    codes = ring.tile([P, N // 2], U32, name="w_codes", align_bytes=64, bufs=8)
                width = P if i >= PASSES and i % PASSES == 0 and u == 0 else N // 2
                for first in range(0, N // 2, width):
                    part = slice(columns.start + first, columns.start + first + width)
                    values = words[:, part, :].rearrange("p c j -> p (c j)")
                    quantize(nc, codes[:, first : first + width], w_scales[:, part], values)
                w_codes[u] = codes
            return w_codes, w_scales

        def multiply(bank, t, slots, i, w_codes, w_scales, start, stop):
            e, o = divmod(i, PASSES)
            g, first = divmod(e * C, GATHER)
            slots = slice(first + slots.start, first + slots.stop)
            nc.tensor.matmul_mx(
                out=bank,
                lhsT=w_codes[t // 2][:, t % 2 * P : (t % 2 + 1) * P].bitcast(FP8X4),
                lhsT_scale=w_scales[:, t * P : (t + 1) * P],
                rhs=slot_words[g, o][:, slots].bitcast(FP8X4),
                rhs_scale=slot_scales[g][4 * o :, slots],
                start=start,
                stop=stop,
            )

        def multiply_chunk(i, w_codes, w_scales):
            e, o = divmod(i, PASSES)
            for u in range(2):
                if e < E - 2:
                    if o == 0:
                        banks[e, u] = psum.tile([P, 2, C], F32, name=f"sums{u}")
                    for v in range(2):
                        start, stop = (o, v) == (0, 0), (o, v) == (PASSES - 1, 1)
                        multiply(banks[e, u][:, v, :], 2 * u + v, slice(0, C), i, w_codes, w_scales, start, stop)
            for h in range(HALVES if e >= E - 2 else 0):
                if o == 0:
                    banks[e, h] = psum.tile([P, PACK, P], F32, name=f"sums{h}")
                tiles = (3, 0, 1, 2) if (i, h) == (LAST, 1) else (0, 1, 2, 3)
                for t in tiles:
                    start, stop = (o, t) == (0, tiles[0]), (o, t) == (PASSES - 1, tiles[-1])
                    multiply(banks[e, h][:, t, :], t, slice(h * P, (h + 1) * P), i, w_codes, w_scales, start, stop)

        def project(bank, r, c_codes, c_scales):
            nc.tensor.matmul_mx(
                out=bank,
                lhsT=wp_codes[:, r * P : (r + 1) * P].bitcast(FP8X4),
                lhsT_scale=wp_scales[:, r * P : (r + 1) * P],
                rhs=c_codes.bitcast(FP8X4),
                rhs_scale=c_scales,
                start=True,
                stop=True,
            )

        def gate_and_project(e):
            c_grouped = keep.tile([P, HALVES, P, PACK], BF16, name="c_grouped", tag="c_bytes", align_bytes=64)
            if e < E - 2:
                pairs = keep.tile([P, 2, C, 2], BF16, name="pairs")
                factors = gates[:, e * HALVES : (e + 1) * HALVES, :].rearrange("p h (c i) -> p (h c) i", i=4)
                for u in range(2):
                    nc.vector.tensor_tensor(
                        pairs[:, u].rearrange("p (c i) v -> p c v i", i=4),
                        banks[e, u][:].rearrange("p v (c i) -> p c v i", i=4),
                        factors.unsqueeze(2).to_broadcast([P, C // 4, 2, 4]),
                        mybir.AluOpType.mult,
                    )
                nc.vector.tensor_copy(
                    out=c_grouped[:].rearrange("p h s t -> p (h s t)").bitcast(F32).rearrange("p (s u) -> p s u", u=2),
                    in_=pairs[:].rearrange("p u s v -> p (u s v)").bitcast(F32).rearrange("p (u s) -> p s u", u=2),
                )
            for h, part in (((), (), ((0, slice(0, P)), (1, slice(0, P))), LAST_PARTS)[e]):
                factors = gates[:, e * HALVES + h, part].rearrange("p (c i) -> p c i", i=2)
                nc.vector.tensor_tensor(
                    c_grouped[:, h, part].rearrange("p (c i) t -> p c t i", i=2),
                    banks[e, h][:, :, part].rearrange("p t (c i) -> p c t i", i=2),
                    factors.unsqueeze(2).to_broadcast([P, (part.stop - part.start) // 2, PACK, 2]),
                    mybir.AluOpType.mult,
                )
            c_codes = ring.tile([P, C], U32, name="c_codes", align_bytes=64, bufs=2)
            c_scales = ring.tile([P, C], U8, name="c_scales", align_bytes=64, bufs=2)
            if e < E - 1:
                for h in range(0, HALVES, HALVES if e < E - 2 else 1):
                    count = HALVES if e < E - 2 else 1
                    slots = slice(h * P, (h + count) * P)
                    values = c_grouped[:, h : h + count].rearrange("p h s t -> p (h s t)")
                    quantize(nc, c_codes[:, slots], c_scales[:, slots], values)
                for r in range(ROW_GROUPS):
                    projected[e, r] = psum.tile([P, C], F32, name="spread", bufs=4)
                    project(projected[e, r][:], r, c_codes[:], c_scales[:])
                return
            results = [keep.tile([P, C], F32, name=f"last_results{r}") for r in range(ROW_GROUPS)]
            for h, part in LAST_PARTS:
                slots = slice(h * P + part.start, h * P + part.stop)
                values = c_grouped[:, h, part].rearrange("p s t -> p (s t)")
                quantize(nc, c_codes[:, slots], c_scales[:, slots], values)
                bank = psum.tile([P, part.stop - part.start], F32, name="spread", bufs=4)
                project(bank[:], 0, c_codes[:, slots], c_scales[:, slots])
                nc.vector.tensor_copy(out=results[0][:, slots], in_=bank[:])
            bank = psum.tile([P, C], F32, name="spread", bufs=4)
            project(bank[:], 1, c_codes[:], c_scales[:])
            nc.scalar.copy(out=results[1][:], in_=bank[:])
            nc.vector.tensor_copy(out=windows[0][:].indirect(slot_offsets(e * C, C)), in_=results[0][:])
            nc.scalar.activation(windows[1][:].indirect(slot_offsets(e * C, C)), results[1][:], COPY)

        def scatter(e, r, results):
            nc.scalar.activation(windows[r][:].indirect(slot_offsets(e * C, C)), results, COPY)

        for g in range(S // GATHER):
            gather_scales(g)
        for i in range(CHUNKS):
            e, o = divmod(i, PASSES)
            grouped = round_chunk(i)
            if i < PASSES:
                gather_words(0, i)
            quantised = quantize_chunk(i, grouped)
            if i < PASSES:
                gather_words(1, i)
            if e > 0 and o == 1:
                groups = range(ROW_GROUPS if e < E - 1 else 1)
                spent = w_raw[i if e < E - 1 else i - 1]
                for r in groups:
                    nc.scalar.copy(out=spent[:, r, N - C : N], in_=projected[e - 1, r][:])
                for r in groups:
                    scatter(e - 1, r, spent[:, r, N - C : N])
            if i == LAST:
                held = w_last[-1][:, 0:2, :].rearrange("p j n -> p (j n)")
                nc.scalar.copy(out=held, in_=projected[E - 2, 1][:])
                scatter(E - 2, 1, held)
            multiply_chunk(i, *quantised)
            if i == 0:
                interleave(nc.scalar.copy, wp_grouped, wp_raw, 0, M)
                quantize(nc, wp_codes[:], wp_scales[:], wp_grouped[:].rearrange("p c j -> p (c j)"))
            if o == PASSES - 1:
                gate_and_project(e)

        for r in range(ROW_GROUPS):
            nc.sync.dma_start(out=out[r * P : (r + 1) * P, :], in_=windows[r][:])
